import numpy as np, ml_dtypes
CORES = [66,74,82,90,194,202,210,218]
N = 8
BF = ml_dtypes.bfloat16
def gentries(a):
    return np.ascontiguousarray(a.reshape(8, 16, -1).transpose(0, 2, 1)).reshape(8, -1)
def gtable(e):
    e = np.asarray(e); return np.ascontiguousarray(e.reshape(8, -1, 16).transpose(0, 2, 1)).reshape(128, -1).astype(np.int32)
W, MA, J, P, T = 1792, 128, 384, 3, 3
def lanes(rng, big=False):
    jm = np.zeros((N, 8, MA), np.int64); lab = np.zeros((N, 8, J), np.int64); nx = np.zeros((N, 8, 16, J), np.int64)
    for q in range(N):
        for g in range(8):
            o = rng.permutation(J); p = rng.permutation(MA)
            tail = p[(MA * rng.random(J - MA) ** 2).astype(np.int64)]
            if big: tail[:] = p[0]
            lb = np.concatenate([np.arange(MA), tail]); s = np.argsort(lb, kind="stable"); cnt = np.bincount(lb, minlength=MA); st = np.add.accumulate(cnt) - cnt
            jm[q, g] = o[:MA]; lab[q, g, o] = lb
            nx[q, g][:, o] = o[s[st[lb] + (cnt[lb] * rng.random((16, J))).astype(np.int64)]]
            if big:
                pos = np.zeros(J, np.int64); pos[s] = np.arange(J) - st[lb[s]]
                nx[q, g][:8, o] = o[s[st[lb] + (pos + 1) % cnt[lb]]]
    return jm, lab, nx
def parts(rng, big=False):
    jm, lab, nx = lanes(rng, big); pal = rng.integers(0, W, (8, 16, MA, 6))
    ga = np.arange(8)[None, :, None, None]; ka = np.arange(16)[None, None, :, None]
    tool = np.where(rng.random((N, 8, 16, J)) < 0.75, pal[ga, ka, lab[:, :, None, :], rng.integers(0, 6, (N, 8, 16, J))], rng.integers(0, W, (N, 8, 16, J)))
    sh = (N, 8, 16, P, MA)
    name = np.where(rng.random(sh) < 0.8, pal[ga[..., None], ka[..., None], np.arange(MA), rng.integers(0, 6, sh)], rng.integers(0, W, sh))
    x = np.clip(rng.integers(0, 256, (N, 8, 1, W)) + rng.integers(-64, 65, (N, 8, 16, W)), 0, 255)
    lm = np.clip(rng.integers(64, 257, (N, 8, 1, J)) + rng.integers(-48, 49, (N, 8, 16, J)), 0, 255)
    return {"jm": jm, "nx": nx, "tool": tool, "name": name, "f": rng.integers(0, J, sh), "x": x, "lm": lm, "sd": rng.integers(0, 256, (N, 8, 16, W)), "rt": rng.integers(0, 65, (N, 8, 16, T))}
def full(a):
    return np.ascontiguousarray(a.reshape(N, 128, -1))
def pack(v):
    b = {k: full(v[k]).astype(np.float32).astype(BF) for k in ("x", "sd", "lm", "rt")}
    return {"xw": b["x"], "sd": b["sd"], "jt": full(4096 * v["nx"] + v["tool"]).astype(np.int32), "lm": b["lm"], "rt": b["rt"],
            "pk": full(4096 * v["f"] + v["name"]).astype(np.int32), "jm": np.stack([gtable(a) for a in v["jm"]])}
def setup_inputs(rng):
    return pack(parts(rng))
def setup_inputs_ties(rng):
    v = parts(rng)
    n = rng.choice(np.array([0, 7, 8, 9, 10, 16]), (N, 8, 1, W)); r = np.argsort(rng.random((N, 8, 16, W)), axis=2)
    v["x"] = 100 + (r < n).astype(np.int64); v["lm"] = np.full((N, 8, 16, J), 100); v["rt"] = rng.integers(0, 3, (N, 8, 16, T))
    v["f"] = rng.choice(np.array([0, J // 2, J - 1]), (N, 8, 16, P, MA))
    v["name"][:, :, :, 1] = np.where(rng.random((N, 8, 16, MA)) < 0.5, v["name"][:, :, :, 0], v["name"][:, :, :, 1])
    return pack(v)
def setup_inputs_crowd(rng):
    v = parts(rng); few = rng.integers(0, W, (8, 24)); ga = np.arange(8)[None, :, None, None]; m = np.arange(MA)
    v["tool"] = few[ga, rng.integers(0, 24, (N, 8, 16, J))]; v["name"] = few[ga[..., None], rng.integers(0, 24, (N, 8, 16, P, MA))]
    v["x"] = rng.choice(np.array([0, 3, 7, 8, 9, 128, 250, 254, 255]), (N, 8, 16, W)); v["rt"] = rng.choice(np.array([0, 1, 5, 64]), (N, 8, 16, T))
    other = np.setdiff1d(np.arange(W), few)
    for q in range(N):
        o = rng.permutation(8)
        g = o[0]; c, d = rng.permutation(other)[:2]
        v["lm"][q, g] = 255; v["tool"][q, g] = d; v["name"][q, g] = c; v["f"][q, g][:, 0] = J - 1; v["x"][q, g][:, c] = rng.integers(32, 256, 16)
        for g, w in ((o[1], 0), (o[2], 255)):
            c, d, e = rng.permutation(other)[:3]; m0 = int(rng.integers(1, 9))
            nm = np.where(m < m0, e, c); goes = (m == m0) == (w == 0)
            v["lm"][q, g] = 255; v["x"][q, g] = w; v["name"][q, g][0] = nm
            v["tool"][q, g][0, v["jm"][q, g]] = np.where(goes, nm, d)
            v["rt"][q, g] = rng.integers(17, 65, (16, T)) if w == 0 else rng.integers(0, 3, (16, T))
        g = o[3]; a = rng.permutation(W)[:17]; k0 = rng.integers(1, 8, MA)
        v["x"][q, g][:, a[0]] = rng.integers(0, 150, 16)
        v["x"][q, g][:, a[1:]] = rng.permuted(np.tile(rng.integers(150, 256, (16, 1)), (1, 16)), axis=0)
        v["tool"][q, g][:, v["jm"][q, g]] = np.where(np.arange(16)[:, None] < k0[None, :], a[0], a[1:][:, None])
    return pack(v)
def setup_inputs_ends(rng):
    v = parts(rng, True); e = np.array([0, 1, W - 2, W - 1])
    v["tool"] = np.where(rng.random((N, 8, 16, J)) < 0.5, rng.choice(e, (N, 8, 16, J)), v["tool"])
    v["name"] = np.where(rng.random((N, 8, 16, P, MA)) < 0.5, rng.choice(e, (N, 8, 16, P, MA)), v["name"])
    v["sd"] = np.where(rng.random((N, 8, 16, W)) < 0.5, rng.choice(np.array([0, 1, 255]), (N, 8, 16, W)), v["sd"])
    v["f"] = np.where(rng.random((N, 8, 16, P, MA)) < 0.5, rng.choice(np.array([0, J - 1]), (N, 8, 16, P, MA)), v["f"])
    return pack(v)
def setup_inputs_calm(rng):
    v = parts(rng); q = rng.permutation(N)
    v["lm"][q[0]] = 255; a = np.take_along_axis(v["tool"][q[0]], v["jm"][q[0]][:, None, :], 2)
    np.put_along_axis(v["name"][q[0]], rng.integers(0, P, (8, 16, 1, MA)), a[:, :, None, :], 2)
    v["lm"][q[1]] = 0; v["x"][q[1]] = np.maximum(v["x"][q[1]], 1)
    v["tool"][q[2]] = 2 * (v["tool"][q[2]] // 2); v["sd"][q[2]] = 2 * (v["sd"][q[2]] // 2); v["name"][q[2]] = 2 * (v["name"][q[2]] // 2) + 1
    return pack(v)
def setup_inputs_spread(rng):
    v = parts(rng)
    v["x"] = np.minimum((np.exp2(8 * rng.random((N, 8, 1, W))) * rng.random((N, 8, 16, W))).astype(np.int64), 255)
    v["lm"] = np.minimum((np.exp2(8 * rng.random((N, 8, 1, J))) * rng.random((N, 8, 16, J))).astype(np.int64), 255)
    v["rt"] = np.minimum(np.exp2(6 * rng.random((N, 8, 16, T))).astype(np.int64), 64)
    v["sd"] = np.minimum(np.exp2(8 * rng.random((N, 8, 16, W))).astype(np.int64), 255)
    v["tool"] = np.where(rng.random((N, 8, 16, J)) < 0.5, np.minimum((W * rng.random((N, 8, 16, J)) ** 3).astype(np.int64), W - 1), v["tool"])
    v["f"] = np.minimum((J * rng.random((N, 8, 16, P, MA)) ** 3).astype(np.int64), J - 1)
    return pack(v)
def check_inputs(d):
    bad = []
    for k, hi in (("xw", 255), ("sd", 255), ("lm", 255), ("rt", 64)):
        v = np.asarray(d[k]).astype(np.float64)
        if not np.all((v >= 0) & (v <= hi) & (v == np.floor(v))): bad.append("range of " + k)
    for k in ("jt", "pk"):
        v = np.asarray(d[k]).astype(np.int64)
        if np.min(v) < 0 or np.max(v) > 4096 * J - 1 or np.max(v & 4095) > W - 1: bad.append("range of " + k)
    if np.min(d["jm"]) < 0 or np.max(d["jm"]) > J - 1: bad.append("range of jm")
    if bad: return bad
    ok = True; nx = np.asarray(d["jt"]).astype(np.int64).reshape(N, 8, 16, J) >> 12
    for q in range(N):
        starts = gentries(np.asarray(d["jm"][q])).astype(np.int64)
        for g in range(8):
            fr = starts[g]; lab = np.full(J, -1)
            if len(np.unique(fr)) < MA: ok = False; continue
            lab[fr] = np.arange(MA)
            while len(fr):
                tg = nx[q, g][:, fr].reshape(-1); lb = np.tile(lab[fr], 16); new = lab[tg] < 0
                lab[tg[new]] = lb[new]
                if np.any(lab[tg] != lb): ok = False; break
                fr = np.unique(tg[new])
    if not ok: bad.append("lanes: a job can be reached from the starting jobs of two machines")
    return bad
def reference(xw, sd, jt, lm, rt, pk, jm):
    x = xw.astype(np.int64).reshape(N, 8, 16, W); s = sd.astype(np.int64).reshape(N, 8, 16, W); lim = lm.astype(np.int64).reshape(N, 8, 16, J); wr = rt.astype(np.int64).reshape(N, 8, 16, T)
    tab = jt.astype(np.int64).reshape(N, 8, 16, J); p = pk.astype(np.int64).reshape(N, 8, 16, P, MA)
    j = np.stack([gentries(a) for a in jm]).astype(np.int64)
    qa = np.arange(N)[:, None, None]; ga = np.arange(8)[None, :, None]
    for t in range(T):
        jj = np.ascontiguousarray(np.broadcast_to(j[:, :, None, :], (N, 8, 16, MA)))
        rec = np.take_along_axis(tab, jj, 3); a = rec & 4095; n = rec >> 12
        xa = np.take_along_axis(x, a.reshape(N, 8, 1, 16 * MA), 3).reshape(N, 8, 16, 16, MA)
        over = xa > np.take_along_axis(lim, jj, 3)[:, :, :, None, :]
        cond = np.add.reduce(over.astype(np.int64), axis=2) >= 9
        ks = np.argmax(np.add.reduce(xa, axis=2), axis=2)[:, :, None]
        b = a + np.take_along_axis(s, a, 3); b = np.where(b >= W, b - W, b)
        n2 = np.take_along_axis(tab, n, 3) >> 12
        a = np.where(cond, b, a); n = np.where(cond, n2, n)
        np.put_along_axis(tab, jj, 4096 * n + a, 3)
        eq = (p & 4095) == a[:, :, :, None]; hit = np.any(eq, axis=3)
        slot = np.where(hit, np.argmax(eq, axis=3), np.argmax(p >> 12, axis=3))[:, :, :, None]
        old = np.take_along_axis(p, slot, 3)[:, :, :, 0]
        send = np.where(hit, p[:, :, :, P - 1], old)
        np.put_along_axis(p, slot, (4096 * n + a)[:, :, :, None], 3)
        p[:, :, :, P - 1] = np.roll(send, 1, axis=0)
        v = np.take_along_axis(np.where(hit, a, old & 4095), ks, 2)[:, :, 0]; up = np.take_along_axis(hit, ks, 2)[:, :, 0]
        j = np.take_along_axis(n, ks, 2)[:, :, 0]
        low = np.full((N, 8, W), MA); np.minimum.at(low, (qa, ga, v), np.arange(MA)[None, None, :])
        wears = np.take_along_axis(up, np.minimum(low, MA - 1), 2)[:, :, None]
        x = np.where((low < MA)[:, :, None], np.where(wears, np.minimum(x + wr[:, :, :, t:t + 1], 255), np.maximum(x - 8, 0)), x)
    return {"yx": x.reshape(N, 128, W).astype(np.float32).astype(BF), "yp": p.reshape(N, 128, P * MA).astype(np.float32)}

@@ -1,0 +1,432 @@
+from concourse.mybir import AluOpType, AxisListType, ActivationFunctionType
+
+A = AluOpType
+CPY = ActivationFunctionType.Copy
+IDN = ActivationFunctionType.Identity
+W, MA, J, NT = 1792, 128, 384, 3
+XV = (112, 40, 40)
+C1 = 8
+
+_B, _H, _F, _I, _U = "bfloat16", "float16", "float32", "int32", "uint16"
+SCRATCH = {}
+for _names, _w, _d in (
+        ("sdt", W, _B), ("xt", W + MA, _B), ("lmt nxt", J, _B), ("rtb", NT, _B), ("rt8", NT, _F),
+        ("jtt pkt tint nint mall", J, _I), ("jmt kgi", 8, _I), ("tool", J, _F), ("jl vl ofl", 8 * NT, _U), ("al nl", 128, _U),
+        ("xa sg ng ov fd", 2048, _B), ("gm", 128, _B), ("af pre key uw um gout gsum msk rm land2", 128, _F),
+        ("lg nb cc nn nh e0 e1 e2 hit hh v0 v1 s0 s1 shf yy yc", 128, _B), ("uh omv vh dup", 128, _H),
+        ("q0 q1 q2 qv m0 m1 m2 mv give0 give1 give2 gcl gmm land0 land1 iot pmi", 128, _I),
+        ("dm vlf off rcf", 8, _F), ("yo ys", 256, _F), ("zer tri", 512, _B), ("rc", 8, _H), ("kg k15", 8, _U), ("e16", 8, _B),
+        ("ones id4m idn4m idb idn id15 idn15 id05 id8k bt bo tie", 128, _B), ("idh id4k id2k c385 c769", 128, _H),
+        ("ep", 160, _B), ("eph", 160, _H), ("gs gsn", 1024, _H)):
+    for _n in _names.split():
+        SCRATCH[_n] = ("sbuf", [128, _w], _d)
+SCRATCH["jt8"] = ("sbuf", [8, 128], _B)
+for _k in range(8):
+    SCRATCH["ps%d" % _k] = ("psum", [128, 512], _F)
+SEMAPHORES = ["sv", "ss", "sp", "sg", "ljm", "ljt", "llm", "lpk", "lrt", "lxw", "lsd", "a0", "a1", "a2", "sent", "ox", "op", "oq"]
+MSK, NOIDX = 2047, 4188159
+
+
+def rank_program(g, core, T, topo):
+    rank = T.rank_of(core)
+    if rank is None:
+        return
+    nxt_core = T.cores[(rank + 1) % len(T.cores)]
+    prv_core = T.cores[(rank - 1) % len(T.cores)]
+    rid, pid = topo.addr(nxt_core, core)
+    mask = topo.mask(core, nxt_core)
+    nrec = len(topo.engines(prv_core, core))
+
+    ENG = {"v": g.vector, "s": g.scalar, "p": g.tensor, "g": g, "y": g.sync}
+    OWN = {"v": "sv", "s": "ss", "p": "sp", "g": "sg"}
+    cnt = {"sv": 0, "ss": 0, "sp": 0, "sg": 0}
+    clk = {e: {} for e in ENG}
+    snap = {}
+    wr, rd, bk = {}, {}, {}
+
+    def wait(e, toks):
+        for tk in sorted(toks, key=lambda q: (-len(snap[q]), q)):
+            sem, val = tk
+            if clk[e].get(sem, 0) >= val:
+                continue
+            if any(o != tk and snap[o].get(sem, 0) >= val and clk[e].get(o[0], 0) < o[1] for o in toks):
+                continue
+            ENG[e].wait_ge(T.sem[sem], val)
+            for a, b in snap[tk].items():
+                if clk[e].get(a, 0) < b:
+                    clk[e][a] = b
+
+    def deps(e, r, w, banks):
+        toks = set()
+        for k in r:
+            if k in wr:
+                toks.add(wr[k][1])
+        for k in w:
+            if k in wr:
+                toks.add(wr[k][1])
+            for e2, tk in rd.get(k, {}).items():
+                if e2 != e:
+                    toks.add(tk)
+        for b in banks:
+            for e2, tk in bk.get(b, {}).items():
+                if e2 != e:
+                    toks.add(tk)
+        if e == "p":
+            toks = {q for q in toks if q[0] != "sp"}
+        return toks
+
+    def note(e, tk, r, w, banks):
+        s = dict(clk[e])
+        if s.get(tk[0], 0) < tk[1]:
+            s[tk[0]] = tk[1]
+        snap[tk] = s
+        for k in w:
+            wr[k] = (e, tk)
+            rd[k] = {}
+        for k in r:
+            rd.setdefault(k, {})[e] = tk
+        for b in banks:
+            bk.setdefault(b, {})[e] = tk
+
+    def op(e, call, r=(), w=(), b=()):
+        wait(e, deps(e, r, w, b))
+        ins = call()
+        sem = OWN[e]
+        cnt[sem] += 1
+        ins.then_inc(T.sem[sem], 1)
+        note(e, (sem, cnt[sem]), r, w, b)
+
+    def dma(e, out, in_, sem, r=(), w=()):
+        wait(e, deps(e, r, w, ()))
+        ENG[e].dma_start(out, in_).then_inc(T.sem[sem], 16)
+        note(e, (sem, 16), r, w, ())
+
+    def res(x):
+        if isinstance(x, str):
+            return T[x][:, :], x, ()
+        if isinstance(x[0], int):
+            return T["ps%d" % x[0]][:, 128 * x[1]:128 * x[1] + 128], "ps%d_%d" % x, (x[0],)
+        return x[0], x[1], ()
+
+    def tt(out, a, b, o, extra=()):
+        (oa, ok, ob), (aa, ak, ab), (ba, bkk, bb) = res(out), res(a), res(b)
+        op("v", lambda: g.vector.tensor_tensor(oa, aa, ba, o), [ak, bkk] + list(extra), [ok], set(ob) | set(ab) | set(bb))
+
+    def ts(out, a, s1, s2, o0, o1=None, extra=()):
+        (oa, ok, ob), (aa, ak, ab) = res(out), res(a)
+        if o1 is None:
+            f = lambda: g.vector.tensor_scalar(oa, aa, s1, None, o0)
+        else:
+            f = lambda: g.vector.tensor_scalar(oa, aa, s1, s2, o0, o1)
+        op("v", f, [ak] + list(extra), [ok], set(ob) | set(ab))
+
+    def cp(out, a, extra=()):
+        (oa, ok, ob), (aa, ak, ab) = res(out), res(a)
+        op("v", lambda: g.vector.tensor_copy(oa, aa), [ak] + list(extra), [ok], set(ob) | set(ab))
+
+    def act(out, a, func=CPY, extra=(), **kw):
+        (oa, ok, ob), (aa, ak, ab) = res(out), res(a)
+        op("s", lambda: g.scalar.activation(oa, aa, func, **kw), [ak] + list(extra), [ok], set(ob) | set(ab))
+
+    def mm(out, l, r, st, sp):
+        (la, lk, _x), (ra, rk, _y) = res(l), res(r)
+        op("p", lambda: g.tensor.matmul(out[0], la, ra, st, sp), [lk, rk], [out[1]], (out[2],))
+
+    def P(p, a=0, b=128, step=1):
+        base = 128 * p[1]
+        return (T["ps%d" % p[0]][:, base + a:base + b:step], "ps%d_%d" % p, p[0])
+
+    def lst(nm, t):
+        return T[nm][:, 8 * t:8 * t + 8]
+
+    dma("y", T.jmt[:, :], T.jm[:, :], "ljm", w=["jmt"])
+    dma("s", T.jtt[:, :], T.jt[:, :], "ljt", w=["jtt"])
+    dma("y", T.xt[:, 0:W], T.xw[:, :], "lxw", w=["xt"])
+    dma("y", T.lmt[:, :], T.lm[:, :], "llm", w=["lmt"])
+    dma("s", T.sdt[:, :], T.sd[:, :], "lsd", w=["sdt"])
+    dma("y", T.rtb[:, :], T.rt[:, :], "lrt", w=["rtb"])
+    dma("y", T.pkt[:, :], T.pk[:, :], "lpk", w=["pkt"])
+
+    def fill(ap, key, c):
+        op("v", lambda: g.vector.memset(ap, c), (), [key])
+
+    def asel(out, in_, pat, cmp_, f, base, cm):
+        op("g", lambda: g.affine_select(T[out][:, :], T[in_][:, :], pat, cmp_, f, base, cm), [in_], [out])
+
+    fill(T.ones[:, :], "ones", 1.0)
+    fill(T.zer[:, :], "zer", 0.0)
+    fill(T.fd[:, :], "fd", 0.0)
+    asel("bt", "ones", [[-16, 8], [0, 16]], A.is_ge, 0.0, 0, 1)
+    asel("bo", "bt", [[16, 8], [0, 16]], A.is_ge, 0.0, 15, -1)
+    asel("idb", "ones", [[-1, 128]], A.is_equal, 0.0, 0, 1)
+    op("g", lambda: g.iota(T.tie[:, :], [[0, 8], [-1, 16]], 15, 0, allow_small_or_imprecise_dtypes=True), (), ["tie"])
+    op("g", lambda: g.iota(T.kgi[:, :], [[1, 8]], 0, 0), (), ["kgi"])
+    op("g", lambda: g.iota(T.iot[:, :], [[-1, 128]], 128, 1), (), ["iot"])
+    op("g", lambda: g.iota(T.rcf[:, :], [[0, 8]], 1792, 1, allow_small_or_imprecise_dtypes=True), (), ["rcf"])
+    asel("tri", "zer", [[0, 4], [-1, 128]], A.is_ge, 4096.0, -1, 1)
+    fill(T.ep[:, :], "ep", 0.0)
+    for k in range(16):
+        op("s", lambda: g.scalar.activation(T.fd[:, 129 * k:128 * k + 128:16], T.idb[:, k:128:16], CPY), ["idb"] + (["fd"] if k == 0 else []), ["fd%d" % k])
+    for nm, c in (("idn", -1.0), ("id15", 1.5), ("idn15", -1.5), ("id05", 0.5), ("id8k", 8192.0), ("id4m", 4194304.0), ("idn4m", -4194304.0)):
+        act(nm, "idb", scale=c)
+    ts("c385", "ones", 385.0, None, A.mult)
+    ts("c769", "ones", 769.0, None, A.mult)
+    op("v", lambda: g.vector.tensor_copy(T.ep[:, 16:144:16], T.bo[:, 0:128:16]), ["bo"], ["ep"])
+    op("v", lambda: g.vector.tensor_scalar(T.e16[:, :], T.bo[:, 0:128:16], 16.0, None, A.mult), ["bo"], ["e16"])
+    for q in range(8):
+        op("v", lambda: g.vector.tensor_scalar(T.gs[:, 128 * q:128 * q + 128], T.ones[:, :], T.bo[:, 16 * q:16 * q + 1], None, A.mult), ["ones", "bo"], ["gs"] if q == 7 else ["gs_%d" % q])
+    ts("msk", "tie", 15.0, None, A.is_lt)
+    op("v", lambda: g.vector.tensor_scalar(T.k15[:, :], T.kgi[:, :], 16.0, 15.0, A.mult, A.add), ["kgi"], ["k15"])
+
+    op("v", lambda: g.vector.tensor_copy(lst("jl", 0), T.jmt[:, :]), ["jmt"], ["jl0"])
+    ts("nint", "jtt", 12, None, A.logical_shift_right)
+    ts("tint", "jtt", 4095, None, A.bitwise_and)
+    ts("nxt", "nint", -192.0, None, A.add)
+    cp("tool", "tint")
+
+    def nexts(h):
+        act((T.ng[:, 1024 * h:1024 * h + 1024], "ng%d" % h), (T.nxt[:, :].indirect(T.nl[:, 64 * h:64 * h + 64]), "nxt"), extra=["nl"])
+
+    def sisters(h):
+        act((T.sg[:, 1024 * h:1024 * h + 1024], "sg%d" % h), (T.sdt[:, :].indirect(T.al[:, 64 * h:64 * h + 64]), "sdt"), extra=["al"])
+
+    def next_lists(t):
+        jk, jl = "jl%d" % t, lst("jl", t)
+        ts("nl", (T.nxt[:, :].indirect(jl), "nxt"), 192.0, None, A.add, extra=[jk])
+        act("nb", (T.nxt[:, :].indirect(jl), "nxt"), extra=[jk])
+        nexts(0)
+
+    def tool_lists(t):
+        jk, jl = "jl%d" % t, lst("jl", t)
+        cp("al", (T.tool[:, :].indirect(jl), "tool"), extra=[jk])
+        act("af", (T.tool[:, :].indirect(jl), "tool"), extra=[jk])
+
+    def limits(t):
+        act("lg", (T.lmt[:, :].indirect(lst("jl", t)), "lmt"), extra=["jl%d" % t])
+
+    def pick(src, piece, h, first):
+        o = P(piece, 64 * h, 64 * h + 64)
+        if first:
+            mm(o, "idn", (T.nb[:, 64 * h:64 * h + 64], "nb"), True, False)
+        for k in range(16):
+            mm(o, (T.fd[:, 128 * k:128 * k + 128], "fd%d" % k), (T[src][:, 1024 * h + k:1024 * h + 1024:16], "%s%d" % (src, h)),
+               k == 0 and not first, k == 15)
+
+    next_lists(0)
+    tool_lists(0)
+    nexts(1)
+    limits(0)
+    ts("gsn", "gs", -1.0, None, A.mult, extra=["gs_%d" % q for q in range(7)])
+    cp("idh", "idb")
+    cp("eph", "ep")
+    ts("id4k", "idb", 4096.0, None, A.mult)
+    ts("id2k", "idb", 2048.0, None, A.mult)
+    ts("pmi", "iot", 15, None, A.bitwise_and)
+    op("v", lambda: g.vector.tensor_tensor(T.rc[:, :], T.rcf[:, :], T.bo[:, 0:128:16], A.mult), ["rcf", "bo"], ["rc"])
+    cp("kg", "kgi")
+    ts("rm", "pmi", 0.0, -1.0, A.is_equal, A.add)
+
+    MN = [(T.mall[:, 0:128], "mall"), (T.mall[:, 128:256], "mall"), (T.mall[:, 256:384], "mall")]
+
+    def first_pockets():
+        ts("mall", "pkt", 4095, None, A.bitwise_and)
+        for i in range(3):
+            ts((0, i), (T.pkt[:, 128 * i:128 * i + 128], "pkt"), 2.0, 2048.0 * (2 - i), A.mult, A.add)
+        for i in range(3):
+            tt("q%d" % i, (0, i), MN[i], A.subtract)
+        tt((0, 0), "q0", "q1", A.max)
+
+    for t in range(NT):
+        last = t == NT - 1
+        jk, jl = "jl%d" % t, lst("jl", t)
+        xv = XV[t]
+        if t:
+            sisters(0)
+        op("v", lambda: g.vector.tensor_copy(T.xa[:, 0:16 * xv], T.xt[:, 0:W].indirect(T.al[:, 0:xv])), ["xt", "al"], ["xa0"])
+        op("s", lambda: g.scalar.activation(T.xa[:, 16 * xv:2048], T.xt[:, 0:W].indirect(T.al[:, xv:128]), CPY), ["xt", "al"], ["xa1"])
+        if t == 0:
+            sisters(0)
+        sisters(1)
+        pick("ng", (4, 0), 0, True)
+        pick("ng", (4, 0), 1, True)
+        mm(P((4, 1)), "idb", "lg", True, True)
+        if t:
+            pick("sg", (3, 0), 0, False)
+        for b in range(2):
+            mm((T["ps%d" % (6 + b)][:, :], "ps%d" % (6 + b), 6 + b), "idb", "tri", True, False)
+        mm(P((1, 0)), "idb", "tie", True, False)
+        for k in range(16):
+            o = P((1, 0), k, 128, 16)
+            op("p", lambda: g.tensor.matmul(o[0], T.xa[:, k:2048:16], T.e16[:, :], False, k == 15), ["xa0", "xa1", "e16"], [o[1]], (1,))
+
+        def beginning():
+            if t == 0:
+                first_pockets()
+                ts("rt8", "rtb", 8.0, None, A.add)
+            else:
+                tt("q0", "q0", (0, 0), A.subtract)
+                tt("q1", "q1", (0, 1), A.subtract)
+                ld = "land%d" % (t - 1)
+                tk = ("a%d" % (t - 1), nrec)
+                snap[tk] = {tk[0]: nrec}
+                wr[ld] = ("r", tk)
+                ts("m0", "q0", MSK, None, A.bitwise_and)
+                ts("m1", "q1", MSK, None, A.bitwise_and)
+                tt((0, 0), "q0", "q1", A.max)
+                ts("q2", ld, NOIDX, None, A.bitwise_and)
+                MN[0], MN[1], MN[2] = "m0", "m1", "m2"
+                ts("m2", ld, MSK, None, A.bitwise_and)
+            tt((0, 1), (0, 0), "q2", A.max)
+            tt("qv", (0, 0), "q2", A.max)
+            tt("v0", "q0", (0, 1), A.is_equal)
+            ts("mv", "qv", MSK, None, A.bitwise_and)
+
+        if t:
+            beginning()
+
+        def compare(k):
+            op("v", lambda: g.vector.tensor_tensor(T.ov[:, 128 * k:128 * k + 128], T.xa[:, k:2048:16], T.ps4[:, 128:256], A.is_gt),
+               ["xa0", "xa1", "ps4_1"], ["ov%d" % k], (4,))
+            mm(P((2, 0)), (T.ep[:, 16 - k:144 - k], "ep"), (T.ov[:, 128 * k:128 * k + 128], "ov%d" % k), k == 0, k == 15)
+
+        for k in range(C1):
+            compare(k)
+        op("v", lambda: g.vector.tensor_tensor_scan(T.pre[:, :], T.msk[:, :], T.ps1[:, 0:128], 0.0, A.mult, A.max), ["msk", "ps1_0"], ["pre"], (1,))
+        cp("key", (1, 0))
+        compare(C1)
+        compare(C1 + 1)
+        tt("gm", (T.pre[:, :].indirect(T.k15[:, :]), "pre"), "key", A.is_equal, extra=["k15"])
+        for k in range(C1 + 2, 12):
+            compare(k)
+        if t == 0:
+            beginning()
+        mm(P((1, 1)), "gm", "idb", True, True)
+        if t == 0:
+            pick("sg", (3, 0), 0, False)
+        for k in range(12, 16):
+            compare(k)
+        tt("omv", "mv", (1, 1), A.mult)
+        ts("cc", (2, 0), 9.0, None, A.is_ge)
+        tt("v1", "q1", (0, 1), A.is_equal)
+        pick("sg", (3, 0), 1, False)
+        tt((4, 2), "cc", (4, 0), A.mult)
+        tt((3, 1), "cc", (3, 0), A.mult)
+        tt("nn", "nb", (4, 2), A.add)
+        tt("uw", "af", (3, 1), A.add)
+        if not last:
+            tt("nh", "nn", (1, 1), A.mult)
+            for r in range(16):
+                mm((T.ps2[0:8, 128 + r:256:16], "ps2_1", 2), (T.nh[:, r:128:16], "nh"), (T.bo[:, 0:128:16], "bo"), True, True)
+        ts((3, 2), "uw", 1792.0, -1792.0, A.is_ge, A.mult)
+        if not last:
+            op("v", lambda: g.vector.tensor_copy(T.nxt[:, :].indirect(jl), T.nn[:, :]), ["nn", jk], ["nxt"])
+        tt((3, 3), "uw", (3, 2), A.add)
+        tt("uh", "uw", (3, 2), A.add)
+        if not last:
+            op("v", lambda: g.vector.tensor_copy(T.jt8[:, :], T.ps2[0:8, 128:256]), ["ps2_1"], ["jt8"], (2,))
+            mm(P((2, 2), 0, 8), "jt8", (T.idb[0:8, 0:8], "idb"), True, True)
+        tt("e0", MN[0], (3, 3), A.is_equal)
+        tt("e1", MN[1], (3, 3), A.is_equal)
+        tt("e2", MN[2], (3, 3), A.is_equal)
+        o = P((5, 3))
+        mm(o, "id4m", "ones", True, False)
+        for x in ("e0", "e1", "e2"):
+            mm(o, "idn4m", x, False, x == "e2")
+        if not last:
+            op("v", lambda: g.vector.tensor_scalar(lst("jl", t + 1), T.ps2[:, 256:264], 192.0, None, A.add), ["ps2_2"], ["jl%d" % (t + 1)], (2,))
+        tt("um", "mv", (3, 3), A.subtract)
+        if not last:
+            next_lists(t + 1)
+        ts("hit", (5, 3), 1.0, None, A.is_lt)
+        tt((3, 1), "um", (1, 1), A.mult)
+        tt("hh", "hit", (1, 1), A.mult)
+        tt((3, 2), "hit", (3, 1), A.mult)
+        tt((0, 3), "q2", (5, 3), A.max)
+        tt("vh", "omv", (3, 2), A.subtract)
+        gv = "give%d" % t
+        if not last:
+            op("v", lambda: g.vector.tensor_copy(T.tool[:, :].indirect(jl), T.uh[:, :]), ["uh", jk], ["tool"])
+        tt(gv, "qv", (0, 3), A.min)
+        for b in range(2):
+            full = (T["ps%d" % (6 + b)][:, :], "ps%d" % (6 + b), 6 + b)
+            for q in range(4):
+                gg = 4 * b + q
+                mm((T["ps%d" % (6 + b)][:, 128 * q:128 * q + 128], "ps%d" % (6 + b), 6 + b), (T.gs[:, 128 * gg:128 * gg + 128], "gs"), "vh", False, False)
+            mm(full, "vh", (T.gsn[:, 512 * b:512 * b + 512], "gsn"), False, True)
+        mm(P((2, 2)), "bo", "hh", True, True)
+        o = P((1, 2), 0, 8)
+        for r in range(16):
+            mm(o, (T.eph[:, 16 - r:144 - r], "eph"), (T.vh[:, r:128:16], "vh"), r == 0, r == 15)
+        o = P((5, 1))
+        mm(o, "id15", "e0", True, False)
+        mm(o, "id05", "v0", False, True)
+        o = P((5, 2))
+        mm(o, "id15", "e1", True, False)
+        mm(o, "idn15", "e0", False, False)
+        mm(o, "id05", "v1", False, True)
+        out = gv
+        if not last:
+            nexts(1)
+        else:
+            ts("gcl", gv, NOIDX, None, A.bitwise_and)
+            ts("gmm", gv, MSK, None, A.bitwise_and)
+            tt("gsum", "gcl", "gmm", A.add)
+        act("shf", (2, 2), IDN, extra=["rt8"], scale=T.rt8[:, t:t + 1], bias=-8.0)
+        if not last:
+            tool_lists(t + 1)
+            limits(t + 1)
+
+        def reduce(gg):
+            b, q = 6 + gg // 4, gg % 4
+            op("v", lambda: g.vector.tensor_reduce(T.dm[:, gg:gg + 1], T["ps%d" % b][:, 128 * q:128 * q + 128], AxisListType.X, A.min, apply_absolute_value=True),
+               ["ps%d" % b], ["dm%d" % gg], (b,))
+
+        for gg in range(4):
+            reduce(gg)
+        if last:
+            ts("gout", "gsum", 0.5, None, A.mult)
+            out = "gout"
+        wait("g", deps("g", [out], (), ()))
+        g.remote_dma(T["land%d" % t][:, :], T[out][:, :], T.sem["a%d" % t], T.sem.sent, pid, rid, mask)
+        for gg in range(4, 8):
+            reduce(gg)
+        vk, ok_ = "vl%d" % t, "ofl%d" % t
+        dmk = ["dm%d" % q for q in range(8)]
+        op("v", lambda: g.vector.tensor_copy(lst("vl", t), T.ps1[:, 256:264]), ["ps1_2"], [vk], (1,))
+        op("v", lambda: g.vector.tensor_copy(T.vlf[:, :], T.ps1[:, 256:264]), ["ps1_2"], ["vlf"], (1,))
+        op("v", lambda: g.vector.tensor_tensor(T.dup[:, :], T.dm[:, :].indirect(T.kg[:, :]), T.rm[:, :], A.is_equal), dmk + ["kg", "rm"], ["dup"])
+        mm((T.ps2[:, 384:392], "ps2_3", 2), "dup", "rc", True, True)
+        for i in range(2):
+            o = P((4, 2 + i))
+            mm(o, "id8k", "nn", True, False)
+            mm(o, "idh", "uh", False, False)
+            mm(o, ("id4k", "id2k")[i], ("c385", "c769")[i], False, True)
+        tt("s0", "hit", (5, 1), A.is_lt)
+        tt("s1", "hit", (5, 2), A.is_lt)
+        tt("yy", (T.xt[:, 0:W].indirect(lst("vl", t)), "xt"), "shf", A.add, extra=[vk])
+        op("v", lambda: g.vector.tensor_tensor(T.off[:, :], T.vlf[:, :], T.ps2[:, 384:392], A.max), ["vlf", "ps2_3"], ["off"], (2,))
+        tt((0, 0), "q0", (4, 2), A.subtract)
+        ts("yc", "yy", 0.0, 255.0, A.max, A.min)
+        op("v", lambda: g.vector.tensor_copy(lst("ofl", t), T.off[:, :]), ["off"], [ok_])
+        tt((0, 1), "q1", (4, 3), A.subtract)
+        op("v", lambda: g.vector.tensor_copy(T.xt[:, :].indirect(lst("ofl", t)), T.yc[:, :]), ["yc", ok_], ["xt"])
+        tt((0, 0), "s0", (0, 0), A.mult)
+        tt((0, 1), "s1", (0, 1), A.mult)
+        if last:
+            dma("y", T.yx[:, :], T.xt[:, 0:W], "ox", r=["xt"])
+            g.scalar.wait_ge(T.sem.a2, nrec)
+            g.scalar.dma_start(T.yp[:, 256:384], T.land2[:, :]).then_inc(T.sem.oq, 16)
+            for i in range(2):
+                tt("q%d" % i, "q%d" % i, (0, i), A.subtract)
+            for i in range(2):
+                ts("m%d" % i, "q%d" % i, MSK, None, A.bitwise_and)
+            for i in range(2):
+                tt((T.ys[:, 128 * i:128 * i + 128], "ys%d" % i), "q%d" % i, "m%d" % i, A.add)
+            for i in range(2):
+                ts((T.yo[:, 128 * i:128 * i + 128], "yo%d" % i), (T.ys[:, 128 * i:128 * i + 128], "ys%d" % i), 0.5, -1024.0 * (2 - i), A.mult, A.add)
+            dma("s", T.yp[:, 0:256], T.yo[:, :], "op", r=["yo0", "yo1"])
+    for sem in ("sv", "ss", "sp", "sg"):
+        g.wait_ge(T.sem[sem], cnt[sem])
+    g.wait_ge(T.sem.sent, NT * len(topo.engines(core, nxt_core)))
+    for sem in ("ox", "op", "oq"):
+        g.wait_ge(T.sem[sem], 16)

@@ -1,30 +1,42 @@
-from concourse.mybir import AluOpType, AxisListType, ActivationFunctionType
+from concourse.bass import DstId, RemoteDMATransfer
+from concourse.mybir import AluOpType, ActivationFunctionType
 
 A = AluOpType
 CPY = ActivationFunctionType.Copy
 IDN = ActivationFunctionType.Identity
+RELU = ActivationFunctionType.Relu
+SIGN = ActivationFunctionType.Sign
 W, MA, J, NT = 1792, 128, 384, 3
-XV = (112, 40, 40)
-C1 = 8
+HALF, QUARTER = (("v", 0, 32), ("s", 64, 128), ("v", 32, 64)), (("v", 0, 32), ("s", 32, 64), ("s", 64, 128))
+XV = (HALF, QUARTER, QUARTER)
+PIECE = 64
+BIG = 4194304.0
+CYCLE, GATHER, SCATTER, LATE, DMA, RATE, FAR = 0.83, 1.1, 2.3, 120, 1500, 450, 5500
+LB = (5, 4, 6, 7)
 
 _B, _H, _F, _I, _U = "bfloat16", "float16", "float32", "int32", "uint16"
 SCRATCH = {}
 for _names, _w, _d in (
-        ("sdt", W, _B), ("xt", W + MA, _B), ("lmt nxt", J, _B), ("rtb", NT, _B), ("rt8", NT, _F),
-        ("jtt pkt tint nint mall", J, _I), ("jmt kgi", 8, _I), ("tool", J, _F), ("jl vl ofl", 8 * NT, _U), ("al nl", 128, _U),
-        ("xa sg ng ov fd", 2048, _B), ("gm", 128, _B), ("af pre key uw um gout gsum msk rm land2", 128, _F),
-        ("lg nb cc nn nh e0 e1 e2 hit hh v0 v1 s0 s1 shf yy yc", 128, _B), ("uh omv vh dup", 128, _H),
-        ("q0 q1 q2 qv m0 m1 m2 mv give0 give1 give2 gcl gmm land0 land1 iot pmi", 128, _I),
-        ("dm vlf off rcf", 8, _F), ("yo ys", 256, _F), ("zer tri", 512, _B), ("rc", 8, _H), ("kg k15", 8, _U), ("e16", 8, _B),
-        ("ones id4m idn4m idb idn id15 idn15 id05 id8k bt bo tie", 128, _B), ("idh id4k id2k c385 c769", 128, _H),
-        ("ep", 160, _B), ("eph", 160, _H), ("gs gsn", 1024, _H)):
+        ("sdt", W, _B), ("xt", W + 8 * MA, _B), ("lmt", J, _B), ("rtb", NT, _B), ("rtn", NT, _F), ("nxt", J, _F),
+        ("jtt pkt tool nint mall qa0 qa1 qa2", J, _I), ("jmt kgi", 8, _I), ("jl vl ofl", 8 * NT, _U), ("anl", 256, _U),
+        ("xa sg ov fd ex zer", 2048, _B), ("ng", 2048, _H), ("gm", 144, _B), ("pre pr2 msk land x1 q2n gw", 128, _F),
+        ("lg lgt cc al be ohs ohm shf yy yc m01", 128, _B), ("ee", 384, _B), ("ss", 256, _B), ("an un", 256, _H),
+        ("j8 v8 uw wf nh omv ohu vh", 128, _H), ("qv mv q2c1 q2c2 g10 g11 h2 hv", 128, _I), ("qm y1 y2 yo", 256, _F),
+        ("qt", 256, _I), ("off spare", 8, _F), ("tri", 512, _B), ("k15", 8, _U), ("c4k", 2, _B),
+        ("ones c50 c25 idb idn id8k id4m idn4m idn8m bt bo", 128, _B),
+        ("ep", 160, _B), ("gs gsn eq", 1024, _B)):
     for _n in _names.split():
         SCRATCH[_n] = ("sbuf", [128, _w], _d)
-SCRATCH["jt8"] = ("sbuf", [8, 128], _B)
 for _k in range(8):
     SCRATCH["ps%d" % _k] = ("psum", [128, 512], _F)
 SEMAPHORES = ["sv", "ss", "sp", "sg", "ljm", "ljt", "llm", "lpk", "lrt", "lxw", "lsd", "a0", "a1", "a2", "sent", "ox", "op", "oq"]
-MSK, NOIDX = 2047, 4188159
+MSK, NOIDX, NOTAG = 2047, 4188159, 4194303
+P01, NP, DN = (0, 0), (0, 1), (3, 1)
+CNT, MISS, AUP, ZL = (1, 0), (1, 1), (1, 2), (1, 3)
+SUM, OH, JL, VL = (2, 0), (2, 1), (2, 2), (2, 3)
+DU, SR, OM = (3, 0), (3, 2), (3, 3)
+UU, SC = (4, 0), (4, 2)
+UN, NQ = (5, 0), (5, 1)
 
 
 def rank_program(g, core, T, topo):
@@ -42,7 +54,27 @@ def rank_program(g, core, T, topo):
     cnt = {"sv": 0, "ss": 0, "sp": 0, "sg": 0}
     clk = {e: {} for e in ENG}
     snap = {}
-    wr, rd, bk = {}, {}, {}
+    calls = []
+    used, turn = {}, {}
+    moved = [0]
+
+    def R(x, a=0, b=None, step=1):
+        if isinstance(x, str):
+            b = SCRATCH[x][1][1] if b is None else b
+            return T[x][:, a:b:step], [(x, frozenset(range(a, b, step)))]
+        if isinstance(x[0], int):
+            base = 128 * x[1]
+            return R("ps%d" % x[0], base + a, base + (128 if b is None else b), step)
+        return x
+
+    def top(x):
+        nm, c = R(x)[1][0]
+        c = sorted(c)
+        return T[nm][0:8, c[0]:c[-1] + 1:c[1] - c[0]], [(nm, frozenset(c))]
+
+    def G(win, off):
+        win, off = R(win), R(off)
+        return win[0].indirect(off[0]), win[1], off[1]
 
     def wait(e, toks):
         for tk in sorted(toks, key=lambda q: (-len(snap[q]), q)):
@@ -56,375 +88,386 @@ def rank_program(g, core, T, topo):
                 if clk[e].get(a, 0) < b:
                     clk[e][a] = b
 
-    def deps(e, r, w, banks):
-        toks = set()
-        for k in r:
-            if k in wr:
-                toks.add(wr[k][1])
-        for k in w:
-            if k in wr:
-                toks.add(wr[k][1])
-            for e2, tk in rd.get(k, {}).items():
-                if e2 != e:
-                    toks.add(tk)
-        for b in banks:
-            for e2, tk in bk.get(b, {}).items():
-                if e2 != e:
-                    toks.add(tk)
-        if e == "p":
-            toks = {q for q in toks if q[0] != "sp"}
-        return toks
+    def op(e, call, outs, ins, busy, late=None, token=None, after=()):
+        acc = []
+        for o in outs:
+            acc += [(nm, c, True) for nm, c in o[1]] + [(nm, c, False) for x in o[2:] for nm, c in x]
+        for o in ins:
+            acc += [(nm, c, False) for x in o[1:] for nm, c in x]
+        me, hard, soft = len(calls), set(after), set()
+        for nm, c, wrt in acc:
+            old = used.get(nm, [])
+            if SCRATCH[nm][0] == "psum":
+                if old and old[-1][0] != me and calls[old[-1][0]]["e"] != e:
+                    turn[nm], old = [u[0] for u in old], []
+                hard.update(turn.get(nm, ()))
+                if e == "p":
+                    soft.update(u[0] for u in old[-1:])
+            for i, c2, wrt2 in old:
+                if i != me and (wrt or wrt2) and c & c2:
+                    same = calls[i]["e"] == e and token is None and calls[i]["token"] is None
+                    (soft if same and (e == "p" or not wrt2) else hard).add(i)
+            used[nm] = [u for u in old if not (wrt and u[1] <= c)] + [(me, c, wrt)]
+        calls.append(dict(e=e, call=call, busy=busy, late=LATE if late is None else late, token=token, hard=hard, soft=soft - hard - {me}))
+        return me
 
-    def note(e, tk, r, w, banks):
-        s = dict(clk[e])
-        if s.get(tk[0], 0) < tk[1]:
-            s[tk[0]] = tk[1]
-        snap[tk] = s
-        for k in w:
-            wr[k] = (e, tk)
-            rd[k] = {}
-        for k in r:
-            rd.setdefault(k, {})[e] = tk
-        for b in banks:
-            bk.setdefault(b, {})[e] = tk
+    def issue():
+        succ = [[] for _ in calls]
+        left = [0] * len(calls)
+        for i, c in enumerate(calls):
+            for j in c["hard"] | c["soft"]:
+                succ[j].append(i)
+                left[i] += 1
+        free = {e: 0.0 for e in "vspgyr"}
+        can = [0.0] * len(calls)
+        ready = [i for i in range(len(calls)) if not left[i]]
+        while ready:
+            start = {i: max(can[i], free[calls[i]["e"]]) for i in ready}
+            first = min(ready, key=lambda i: (start[i], i))
+            i = min([first] + [i for i in ready if calls[i]["e"] == calls[first]["e"] and start[i] < start[first] + calls[first]["busy"]])
+            ready.remove(i)
+            c = calls[i]
+            e = c["e"]
+            free[e] = start[i] + c["busy"]
+            for j in succ[i]:
+                can[j] = max(can[j], free[e] + (c["late"] if i in calls[j]["hard"] else 0))
+                left[j] -= 1
+                if not left[j]:
+                    ready.append(j)
+            known = {}
+            if e != "r":
+                wait(e, {calls[j]["token"] for j in c["hard"]})
+                ins = c["call"]()
+                if c["token"] is None:
+                    cnt[OWN[e]] += 1
+                    c["token"] = (OWN[e], cnt[OWN[e]])
+                    ins.then_inc(T.sem[OWN[e]], 1)
+                known = dict(clk[e])
+            if c["token"]:
+                known[c["token"][0]] = c["token"][1]
+                snap[c["token"]] = known
 
-    def op(e, call, r=(), w=(), b=()):
-        wait(e, deps(e, r, w, b))
-        ins = call()
-        sem = OWN[e]
-        cnt[sem] += 1
-        ins.then_inc(T.sem[sem], 1)
-        note(e, (sem, cnt[sem]), r, w, b)
+    def load(e, nm, src, sem, b=None):
+        o = R(nm, 0, b)
+        moved[0] += 128 * len(o[1][0][1]) * (4 if SCRATCH[nm][2] == _I else 2)
+        op(e, lambda: ENG[e].dma_start(o[0], src[:, :]).then_inc(T.sem[sem], 16), [o], [], 60, DMA + moved[0] / RATE, (sem, 16))
+        calls[-1]["soft"].update(range(len(calls) - 1))
 
-    def dma(e, out, in_, sem, r=(), w=()):
-        wait(e, deps(e, r, w, ()))
-        ENG[e].dma_start(out, in_).then_inc(T.sem[sem], 16)
-        note(e, (sem, 16), r, w, ())
+    def store(e, dst, x, sem):
+        op(e, lambda: ENG[e].dma_start(dst, x[0]).then_inc(T.sem[sem], 16), [], [x], 60, DMA, (sem, 16))
 
-    def res(x):
-        if isinstance(x, str):
-            return T[x][:, :], x, ()
-        if isinstance(x[0], int):
-            return T["ps%d" % x[0]][:, 128 * x[1]:128 * x[1] + 128], "ps%d_%d" % x, (x[0],)
-        return x[0], x[1], ()
+    def give(t, a, b, fold, dst):
+        a, b, dst = R(a), R(b), R(dst)
+        move = RemoteDMATransfer(dst_ids=[DstId(rid=rid, pnc=pid)], dma_engine_mask=mask, remote_sem=T.sem["a%d" % t],
+                                 srcs=[a[0], b[0]], dsts=[dst[0]], alu_op=fold)
+        i = op("g", lambda: g.remote_dma_fused([move], local_sem=T.sem.sent), [], [a, b], 100, FAR, False)
+        op("r", None, [dst], [], 0, 0, ("a%d" % t, nrec), [i])
 
-    def tt(out, a, b, o, extra=()):
-        (oa, ok, ob), (aa, ak, ab), (ba, bkk, bb) = res(out), res(a), res(b)
-        op("v", lambda: g.vector.tensor_tensor(oa, aa, ba, o), [ak, bkk] + list(extra), [ok], set(ob) | set(ab) | set(bb))
+    def time(out, ins, per):
+        n = len(out[1][0][1]) if len(out) == 2 else 16 * len(out[2][0][1])
+        if len(out) > 2:
+            return 60 + n * SCATTER
+        return 60 + n * GATHER if len(ins[0]) > 2 else 10 + max(64, n * per) * CYCLE
 
-    def ts(out, a, s1, s2, o0, o1=None, extra=()):
-        (oa, ok, ob), (aa, ak, ab) = res(out), res(a)
-        if o1 is None:
-            f = lambda: g.vector.tensor_scalar(oa, aa, s1, None, o0)
-        else:
-            f = lambda: g.vector.tensor_scalar(oa, aa, s1, s2, o0, o1)
-        op("v", f, [ak] + list(extra), [ok], set(ob) | set(ab))
+    def short(*xs):
+        return 0.5 if all(SCRATCH[x[1][0][0]][2] in (_B, _H, _U) for x in xs) else 1
 
-    def cp(out, a, extra=()):
-        (oa, ok, ob), (aa, ak, ab) = res(out), res(a)
-        op("v", lambda: g.vector.tensor_copy(oa, aa), [ak] + list(extra), [ok], set(ob) | set(ab))
+    def col(x):
+        return x[0] if isinstance(x, tuple) else x
 
-    def act(out, a, func=CPY, extra=(), **kw):
-        (oa, ok, ob), (aa, ak, ab) = res(out), res(a)
-        op("s", lambda: g.scalar.activation(oa, aa, func, **kw), [ak] + list(extra), [ok], set(ob) | set(ab))
+    def cols(*xs):
+        return [x for x in xs if isinstance(x, tuple)]
+
+    def tt(out, a, b, o):
+        out, a, b = R(out), R(a), R(b)
+        both = SCRATCH[a[1][0][0]][0] == SCRATCH[b[1][0][0]][0]
+        op("v", lambda: g.vector.tensor_tensor(out[0], a[0], b[0], o), [out], [a, b], time(out, [a], 1 + both))
+
+    def ts(out, a, s1, s2, *o):
+        out, a = R(out), R(a)
+        op("v", lambda: g.vector.tensor_scalar(out[0], a[0], col(s1), col(s2), *o), [out], [a] + cols(s1, s2), time(out, [a], short(out, a)))
+
+    def cp(out, a):
+        out, a = R(out), R(a)
+        op("v", lambda: g.vector.tensor_copy(out[0], a[0]), [out], [a], time(out, [a], short(out, a)))
+
+    def scan(out, a, b):
+        out, a, b = R(out), R(a), R(b)
+        op("v", lambda: g.vector.tensor_tensor_scan(out[0], a[0], b[0], 0.0, A.mult, A.max), [out], [a, b], time(out, [a], 1))
+
+    def act(out, a, func=CPY, bias=0.0, scale=1.0):
+        out, a = R(out), R(a)
+        op("s", lambda: g.scalar.activation(out[0], a[0], func, bias=col(bias), scale=col(scale)), [out], [a] + cols(bias, scale),
+           (75 if len(a) == 2 else 120) + time(out, [a], 1))
 
     def mm(out, l, r, st, sp):
-        (la, lk, _x), (ra, rk, _y) = res(l), res(r)
-        op("p", lambda: g.tensor.matmul(out[0], la, ra, st, sp), [lk, rk], [out[1]], (out[2],))
+        out, l, r = R(out), R(l), R(r)
+        op("p", lambda: g.tensor.matmul(out[0], l[0], r[0], st, sp), [out], [l, r], 3 + max(min(64, len(l[1][0][1])), len(r[1][0][1])) * CYCLE / 2)
 
-    def P(p, a=0, b=128, step=1):
-        base = 128 * p[1]
-        return (T["ps%d" % p[0]][:, base + a:base + b:step], "ps%d_%d" % p, p[0])
+    def lin(out, terms, st=True, sp=True):
+        for i, (l, r) in enumerate(terms):
+            mm(out, l, r, st and i == 0, sp and i == len(terms) - 1)
 
-    def lst(nm, t):
-        return T[nm][:, 8 * t:8 * t + 8]
-
-    dma("y", T.jmt[:, :], T.jm[:, :], "ljm", w=["jmt"])
-    dma("s", T.jtt[:, :], T.jt[:, :], "ljt", w=["jtt"])
-    dma("y", T.xt[:, 0:W], T.xw[:, :], "lxw", w=["xt"])
-    dma("y", T.lmt[:, :], T.lm[:, :], "llm", w=["lmt"])
-    dma("s", T.sdt[:, :], T.sd[:, :], "lsd", w=["sdt"])
-    dma("y", T.rtb[:, :], T.rt[:, :], "lrt", w=["rtb"])
-    dma("y", T.pkt[:, :], T.pk[:, :], "lpk", w=["pkt"])
-
-    def fill(ap, key, c):
-        op("v", lambda: g.vector.memset(ap, c), (), [key])
+    def fill(x, c):
+        x = R(x)
+        op("v", lambda: g.vector.memset(x[0], c), [x], [], time(x, [x], short(x)))
 
     def asel(out, in_, pat, cmp_, f, base, cm):
-        op("g", lambda: g.affine_select(T[out][:, :], T[in_][:, :], pat, cmp_, f, base, cm), [in_], [out])
+        out, in_ = R(out), R(in_)
+        op("g", lambda: g.affine_select(out[0], in_[0], pat, cmp_, f, base, cm), [out], [in_], 150 + time(out, [in_], 2))
 
-    fill(T.ones[:, :], "ones", 1.0)
-    fill(T.zer[:, :], "zer", 0.0)
-    fill(T.fd[:, :], "fd", 0.0)
+    def iota(out, pat, base, cm):
+        o = R(out)
+        op("g", lambda: g.iota(o[0], pat, base, cm, allow_small_or_imprecise_dtypes=SCRATCH[out][2] != _I), [o], [], 150)
+
+    def blk(x, i, n=1):
+        return R(x, 128 * i, 128 * (i + n))
+
+    def lst(nm, t):
+        return R(nm, 8 * t, 8 * t + 8)
+
+    XW = R("xt", 0, W)
+    AL, NL, AH, NH = blk("anl", 0), blk("anl", 1), blk("an", 0), blk("an", 1)
+    E = [blk("ee", i) for i in range(3)]
+    GROUPS = R("bo", 0, 128, 16)
+
+    load("y", "jmt", T.jm, "ljm")
+    load("s", "jtt", T.jt, "ljt")
+    load("s", "lmt", T.lm, "llm")
+    load("y", "xt", T.xw, "lxw", W)
+    load("y", "sdt", T.sd, "lsd")
+    load("s", "pkt", T.pk, "lpk")
+    load("y", "rtb", T.rt, "lrt")
+
+    fill("ones", 1.0)
+    asel("idb", "ones", [[-1, 128]], A.is_equal, 0.0, 0, 1)
     asel("bt", "ones", [[-16, 8], [0, 16]], A.is_ge, 0.0, 0, 1)
     asel("bo", "bt", [[16, 8], [0, 16]], A.is_ge, 0.0, 15, -1)
-    asel("idb", "ones", [[-1, 128]], A.is_equal, 0.0, 0, 1)
-    op("g", lambda: g.iota(T.tie[:, :], [[0, 8], [-1, 16]], 15, 0, allow_small_or_imprecise_dtypes=True), (), ["tie"])
-    op("g", lambda: g.iota(T.kgi[:, :], [[1, 8]], 0, 0), (), ["kgi"])
-    op("g", lambda: g.iota(T.iot[:, :], [[-1, 128]], 128, 1), (), ["iot"])
-    op("g", lambda: g.iota(T.rcf[:, :], [[0, 8]], 1792, 1, allow_small_or_imprecise_dtypes=True), (), ["rcf"])
-    asel("tri", "zer", [[0, 4], [-1, 128]], A.is_ge, 4096.0, -1, 1)
-    fill(T.ep[:, :], "ep", 0.0)
-    for k in range(16):
-        op("s", lambda: g.scalar.activation(T.fd[:, 129 * k:128 * k + 128:16], T.idb[:, k:128:16], CPY), ["idb"] + (["fd"] if k == 0 else []), ["fd%d" % k])
-    for nm, c in (("idn", -1.0), ("id15", 1.5), ("idn15", -1.5), ("id05", 0.5), ("id8k", 8192.0), ("id4m", 4194304.0), ("idn4m", -4194304.0)):
-        act(nm, "idb", scale=c)
-    ts("c385", "ones", 385.0, None, A.mult)
-    ts("c769", "ones", 769.0, None, A.mult)
-    op("v", lambda: g.vector.tensor_copy(T.ep[:, 16:144:16], T.bo[:, 0:128:16]), ["bo"], ["ep"])
-    op("v", lambda: g.vector.tensor_scalar(T.e16[:, :], T.bo[:, 0:128:16], 16.0, None, A.mult), ["bo"], ["e16"])
-    for q in range(8):
-        op("v", lambda: g.vector.tensor_scalar(T.gs[:, 128 * q:128 * q + 128], T.ones[:, :], T.bo[:, 16 * q:16 * q + 1], None, A.mult), ["ones", "bo"], ["gs"] if q == 7 else ["gs_%d" % q])
-    ts("msk", "tie", 15.0, None, A.is_lt)
-    op("v", lambda: g.vector.tensor_scalar(T.k15[:, :], T.kgi[:, :], 16.0, 15.0, A.mult, A.add), ["kgi"], ["k15"])
+    fill("fd", 0.0)
+    fill("zer", 0.0)
+    fill("ep", 0.0)
+    iota("kgi", [[16, 8]], 15, 0)
+    asel("msk", "ones", [[0, 8], [1, 16]], A.is_gt, 0.0, 0, 0)
+    asel("gsn", R("zer", 0, 1024), [[16, 8], [0, 128]], A.is_gt, -1.0, 0, -1)
+    asel("gsn", "gsn", [[16, 8], [0, 128]], A.is_ge, 0.0, 15, -1)
+    asel("tri", R("zer", 0, 512), [[0, 4], [1, 128]], A.is_gt, 0.5, 0, -1)
+    iota("spare", [[1, 8]], W, 8)
+    asel("ex", "zer", [[-1, 128], [0, 16]], A.not_equal, 1.0, 0, 1)
 
-    op("v", lambda: g.vector.tensor_copy(lst("jl", 0), T.jmt[:, :]), ["jmt"], ["jl0"])
-    ts("nint", "jtt", 12, None, A.logical_shift_right)
-    ts("tint", "jtt", 4095, None, A.bitwise_and)
-    ts("nxt", "nint", -192.0, None, A.add)
-    cp("tool", "tint")
+    def next_list(t):
+        cp(NL, G("nxt", lst("jl", t)))
 
-    def nexts(h):
-        act((T.ng[:, 1024 * h:1024 * h + 1024], "ng%d" % h), (T.nxt[:, :].indirect(T.nl[:, 64 * h:64 * h + 64]), "nxt"), extra=["nl"])
+    def tool_list(t):
+        cp(AL, G("tool", lst("jl", t)))
 
-    def sisters(h):
-        act((T.sg[:, 1024 * h:1024 * h + 1024], "sg%d" % h), (T.sdt[:, :].indirect(T.al[:, 64 * h:64 * h + 64]), "sdt"), extra=["al"])
+    def nexts(a, b):
+        for c in range(a, b, PIECE):
+            act(R("ng", 16 * c, 16 * (c + PIECE)), G("nxt", R("anl", 128 + c, 128 + c + PIECE)))
 
-    def next_lists(t):
-        jk, jl = "jl%d" % t, lst("jl", t)
-        ts("nl", (T.nxt[:, :].indirect(jl), "nxt"), 192.0, None, A.add, extra=[jk])
-        act("nb", (T.nxt[:, :].indirect(jl), "nxt"), extra=[jk])
-        nexts(0)
+    def sisters():
+        for c in range(0, 128, PIECE):
+            act(R("sg", 16 * c, 16 * (c + PIECE)), G("sdt", R("anl", c, c + PIECE)))
 
-    def tool_lists(t):
-        jk, jl = "jl%d" % t, lst("jl", t)
-        cp("al", (T.tool[:, :].indirect(jl), "tool"), extra=[jk])
-        act("af", (T.tool[:, :].indirect(jl), "tool"), extra=[jk])
+    def wear(e, a, b):
+        e(R("xa", 16 * a, 16 * b), G(XW, R("anl", a, b)))
 
     def limits(t):
-        act("lg", (T.lmt[:, :].indirect(lst("jl", t)), "lmt"), extra=["jl%d" % t])
+        act("lg", G("lmt", lst("jl", t)))
+        if t:
+            mm(OM, "lg", "idb", True, True)
+            act("lgt", OM)
+
+    def spread(t, b):
+        if t:
+            mm("ps%d" % LB[b], "lgt", R("ex", 512 * b, 512 * b + 512), True, True)
+        for k in range(0 if t else 16):
+            mm(R("ps%d" % LB[b], k, 512, 16), "idb", R("lg", 32 * b, 32 * b + 32), True, True)
+
+    def compare(b):
+        tt(R("ov", 512 * b, 512 * b + 512), R("xa", 512 * b, 512 * b + 512), "ps%d" % LB[b], A.is_gt)
+
+    def count(h):
+        lin(R(CNT, 64 * h, 64 * h + 64), [(R("ep", 16 - k, 144 - k), R("ov", 1024 * h + k, 1024 * h + 1024, 16)) for k in range(16)])
 
     def pick(src, piece, h, first):
-        o = P(piece, 64 * h, 64 * h + 64)
-        if first:
-            mm(o, "idn", (T.nb[:, 64 * h:64 * h + 64], "nb"), True, False)
-        for k in range(16):
-            mm(o, (T.fd[:, 128 * k:128 * k + 128], "fd%d" % k), (T[src][:, 1024 * h + k:1024 * h + 1024:16], "%s%d" % (src, h)),
-               k == 0 and not first, k == 15)
+        o = R(piece, 64 * h, 64 * h + 64)
+        lin(o, first + [(blk("fd", k), R(src, 1024 * h + k, 1024 * h + 1024, 16)) for k in range(16)])
 
-    next_lists(0)
-    tool_lists(0)
-    nexts(1)
-    limits(0)
-    ts("gsn", "gs", -1.0, None, A.mult, extra=["gs_%d" % q for q in range(7)])
-    cp("idh", "idb")
-    cp("eph", "ep")
-    ts("id4k", "idb", 4096.0, None, A.mult)
-    ts("id2k", "idb", 2048.0, None, A.mult)
-    ts("pmi", "iot", 15, None, A.bitwise_and)
-    op("v", lambda: g.vector.tensor_tensor(T.rc[:, :], T.rcf[:, :], T.bo[:, 0:128:16], A.mult), ["rcf", "bo"], ["rc"])
-    cp("kg", "kgi")
-    ts("rm", "pmi", 0.0, -1.0, A.is_equal, A.add)
-
-    MN = [(T.mall[:, 0:128], "mall"), (T.mall[:, 128:256], "mall"), (T.mall[:, 256:384], "mall")]
+    def consts():
+        for nm, c in (("idn", -1.0), ("id4m", BIG), ("idn8m", -2 * BIG), ("id8k", 8192.0), ("idn4m", -BIG)):
+            ts(nm, "idb", c, None, A.mult)
+        ts("gs", "gsn", -1.0, None, A.mult)
+        ts("rtn", "rtb", -1.0, -8.0, A.mult, A.add)
+        for nm, c in (("c50", 0.5), ("c25", 0.25), ("c4k", 4096.0)):
+            fill(nm, c)
 
     def first_pockets():
         ts("mall", "pkt", 4095, None, A.bitwise_and)
         for i in range(3):
-            ts((0, i), (T.pkt[:, 128 * i:128 * i + 128], "pkt"), 2.0, 2048.0 * (2 - i), A.mult, A.add)
-        for i in range(3):
-            tt("q%d" % i, (0, i), MN[i], A.subtract)
-        tt((0, 0), "q0", "q1", A.max)
+            ts((0, i), blk("pkt", i), 2.0, 2048.0 * (2 - i), A.mult, A.add)
+        tt("qa0", R(P01, 0, 384), "mall", A.subtract)
+
+    def update(t):
+        tt("qt", R(NP, 0, 256), blk("qa%d" % t, 0, 2), A.max)
+        ts(blk("qa%d" % (t + 1), 0, 2), "qt", NOTAG, None, A.bitwise_and)
+
+    def arrived(t):
+        qa = "qa%d" % t
+        ts(blk("mall", 0, 2), blk(qa, 0, 2), MSK, None, A.bitwise_and)
+        ts(blk("mall", 2), blk(qa, 2), MSK, None, A.bitwise_and)
+        ts("q2c%d" % t, blk(qa, 2), NOIDX, None, A.bitwise_and)
+
+    def evicted(t, q2):
+        tt("qv", P01, q2, A.max)
+        ts("mv", "qv", MSK, None, A.bitwise_and)
+        tt("al", P01, blk("qa%d" % t, 0), A.not_equal)
+        tt("be", P01, q2, A.is_gt)
+
+    cp(lst("jl", 0), "jmt")
+    ts("tool", "jtt", 4095, None, A.bitwise_and)
+    tool_list(0)
+    limits(0)
+    cp(R("ep", 16, 144, 16), GROUPS)
+    cp("k15", "kgi")
+    fill(R("gm", 0, 16), 1.0)
+    for b in range(4):
+        spread(0, b)
+    for k in range(16):
+        act(R("fd", 129 * k, 128 * k + 128, 16), R("idb", k, 128, 16))
 
     for t in range(NT):
         last = t == NT - 1
-        jk, jl = "jl%d" % t, lst("jl", t)
-        xv = XV[t]
-        if t:
-            sisters(0)
-        op("v", lambda: g.vector.tensor_copy(T.xa[:, 0:16 * xv], T.xt[:, 0:W].indirect(T.al[:, 0:xv])), ["xt", "al"], ["xa0"])
-        op("s", lambda: g.scalar.activation(T.xa[:, 16 * xv:2048], T.xt[:, 0:W].indirect(T.al[:, xv:128]), CPY), ["xt", "al"], ["xa1"])
+        jl, qa = lst("jl", t), "qa%d" % t
+        q2 = R("q2c%d" % t) if t else blk(qa, 2)
+        for e, a, b in XV[t]:
+            wear(cp if e == "v" else act, a, b)
         if t == 0:
-            sisters(0)
-        sisters(1)
-        pick("ng", (4, 0), 0, True)
-        pick("ng", (4, 0), 1, True)
-        mm(P((4, 1)), "idb", "lg", True, True)
-        if t:
-            pick("sg", (3, 0), 0, False)
-        for b in range(2):
-            mm((T["ps%d" % (6 + b)][:, :], "ps%d" % (6 + b), 6 + b), "idb", "tri", True, False)
-        mm(P((1, 0)), "idb", "tie", True, False)
+            ts("nint", "jtt", 12, None, A.logical_shift_right)
+            cp("nxt", "nint")
+            next_list(0)
+            cp("an", "anl")
+        compare(0)
+        compare(1)
+        count(0)
+        compare(2)
+        compare(3)
+        count(1)
         for k in range(16):
-            o = P((1, 0), k, 128, 16)
-            op("p", lambda: g.tensor.matmul(o[0], T.xa[:, k:2048:16], T.e16[:, :], False, k == 15), ["xa0", "xa1", "e16"], [o[1]], (1,))
-
-        def beginning():
-            if t == 0:
-                first_pockets()
-                ts("rt8", "rtb", 8.0, None, A.add)
-            else:
-                tt("q0", "q0", (0, 0), A.subtract)
-                tt("q1", "q1", (0, 1), A.subtract)
-                ld = "land%d" % (t - 1)
-                tk = ("a%d" % (t - 1), nrec)
-                snap[tk] = {tk[0]: nrec}
-                wr[ld] = ("r", tk)
-                ts("m0", "q0", MSK, None, A.bitwise_and)
-                ts("m1", "q1", MSK, None, A.bitwise_and)
-                tt((0, 0), "q0", "q1", A.max)
-                ts("q2", ld, NOIDX, None, A.bitwise_and)
-                MN[0], MN[1], MN[2] = "m0", "m1", "m2"
-                ts("m2", ld, MSK, None, A.bitwise_and)
-            tt((0, 1), (0, 0), "q2", A.max)
-            tt("qv", (0, 0), "q2", A.max)
-            tt("v0", "q0", (0, 1), A.is_equal)
-            ts("mv", "qv", MSK, None, A.bitwise_and)
-
+            mm(R(SUM, k, 128, 16), R("xa", k, 2048, 16), GROUPS, True, True)
+        ts("cc", CNT, 9.0, None, A.is_ge)
+        sisters()
+        pick("sg", DU, 0, [])
+        pick("sg", DU, 1, [])
+        tt(DU, "cc", DU, A.mult)
+        tt("uw", AH, DU, A.add)
+        ts("wf", "uw", float(W), -float(W), A.is_ge, A.mult)
+        lin(UU, [("idb", "uw"), ("idb", "wf")])
+        for pre in ("pre", "pr2"):
+            scan(pre, "msk", SUM)
+        tt(R("gm", 16, 144), G("pre", "k15"), "pr2", A.is_equal)
+        if t == 0:
+            consts()
+        lin(OH, [(R("gm", 16, 144), "idb"), (R("gm", 15, 143), "idn"), (blk("fd", 0), "ones")])
+        act("ohs", OH)
         if t:
-            beginning()
-
-        def compare(k):
-            op("v", lambda: g.vector.tensor_tensor(T.ov[:, 128 * k:128 * k + 128], T.xa[:, k:2048:16], T.ps4[:, 128:256], A.is_gt),
-               ["xa0", "xa1", "ps4_1"], ["ov%d" % k], (4,))
-            mm(P((2, 0)), (T.ep[:, 16 - k:144 - k], "ep"), (T.ov[:, 128 * k:128 * k + 128], "ov%d" % k), k == 0, k == 15)
-
-        for k in range(C1):
-            compare(k)
-        op("v", lambda: g.vector.tensor_tensor_scan(T.pre[:, :], T.msk[:, :], T.ps1[:, 0:128], 0.0, A.mult, A.max), ["msk", "ps1_0"], ["pre"], (1,))
-        cp("key", (1, 0))
-        compare(C1)
-        compare(C1 + 1)
-        tt("gm", (T.pre[:, :].indirect(T.k15[:, :]), "pre"), "key", A.is_equal, extra=["k15"])
-        for k in range(C1 + 2, 12):
-            compare(k)
-        if t == 0:
-            beginning()
-        mm(P((1, 1)), "gm", "idb", True, True)
-        if t == 0:
-            pick("sg", (3, 0), 0, False)
-        for k in range(12, 16):
-            compare(k)
-        tt("omv", "mv", (1, 1), A.mult)
-        ts("cc", (2, 0), 9.0, None, A.is_ge)
-        tt("v1", "q1", (0, 1), A.is_equal)
-        pick("sg", (3, 0), 1, False)
-        tt((4, 2), "cc", (4, 0), A.mult)
-        tt((3, 1), "cc", (3, 0), A.mult)
-        tt("nn", "nb", (4, 2), A.add)
-        tt("uw", "af", (3, 1), A.add)
-        if not last:
-            tt("nh", "nn", (1, 1), A.mult)
-            for r in range(16):
-                mm((T.ps2[0:8, 128 + r:256:16], "ps2_1", 2), (T.nh[:, r:128:16], "nh"), (T.bo[:, 0:128:16], "bo"), True, True)
-        ts((3, 2), "uw", 1792.0, -1792.0, A.is_ge, A.mult)
-        if not last:
-            op("v", lambda: g.vector.tensor_copy(T.nxt[:, :].indirect(jl), T.nn[:, :]), ["nn", jk], ["nxt"])
-        tt((3, 3), "uw", (3, 2), A.add)
-        tt("uh", "uw", (3, 2), A.add)
-        if not last:
-            op("v", lambda: g.vector.tensor_copy(T.jt8[:, :], T.ps2[0:8, 128:256]), ["ps2_1"], ["jt8"], (2,))
-            mm(P((2, 2), 0, 8), "jt8", (T.idb[0:8, 0:8], "idb"), True, True)
-        tt("e0", MN[0], (3, 3), A.is_equal)
-        tt("e1", MN[1], (3, 3), A.is_equal)
-        tt("e2", MN[2], (3, 3), A.is_equal)
-        o = P((5, 3))
-        mm(o, "id4m", "ones", True, False)
-        for x in ("e0", "e1", "e2"):
-            mm(o, "idn4m", x, False, x == "e2")
-        if not last:
-            op("v", lambda: g.vector.tensor_scalar(lst("jl", t + 1), T.ps2[:, 256:264], 192.0, None, A.add), ["ps2_2"], ["jl%d" % (t + 1)], (2,))
-        tt("um", "mv", (3, 3), A.subtract)
-        if not last:
-            next_lists(t + 1)
-        ts("hit", (5, 3), 1.0, None, A.is_lt)
-        tt((3, 1), "um", (1, 1), A.mult)
-        tt("hh", "hit", (1, 1), A.mult)
-        tt((3, 2), "hit", (3, 1), A.mult)
-        tt((0, 3), "q2", (5, 3), A.max)
-        tt("vh", "omv", (3, 2), A.subtract)
-        gv = "give%d" % t
-        if not last:
-            op("v", lambda: g.vector.tensor_copy(T.tool[:, :].indirect(jl), T.uh[:, :]), ["uh", jk], ["tool"])
-        tt(gv, "qv", (0, 3), A.min)
-        for b in range(2):
-            full = (T["ps%d" % (6 + b)][:, :], "ps%d" % (6 + b), 6 + b)
-            for q in range(4):
-                gg = 4 * b + q
-                mm((T["ps%d" % (6 + b)][:, 128 * q:128 * q + 128], "ps%d" % (6 + b), 6 + b), (T.gs[:, 128 * gg:128 * gg + 128], "gs"), "vh", False, False)
-            mm(full, "vh", (T.gsn[:, 512 * b:512 * b + 512], "gsn"), False, True)
-        mm(P((2, 2)), "bo", "hh", True, True)
-        o = P((1, 2), 0, 8)
-        for r in range(16):
-            mm(o, (T.eph[:, 16 - r:144 - r], "eph"), (T.vh[:, r:128:16], "vh"), r == 0, r == 15)
-        o = P((5, 1))
-        mm(o, "id15", "e0", True, False)
-        mm(o, "id05", "v0", False, True)
-        o = P((5, 2))
-        mm(o, "id15", "e1", True, False)
-        mm(o, "idn15", "e0", False, False)
-        mm(o, "id05", "v1", False, True)
-        out = gv
-        if not last:
-            nexts(1)
+            update(t - 1)
         else:
-            ts("gcl", gv, NOIDX, None, A.bitwise_and)
-            ts("gmm", gv, MSK, None, A.bitwise_and)
-            tt("gsum", "gcl", "gmm", A.add)
-        act("shf", (2, 2), IDN, extra=["rt8"], scale=T.rt8[:, t:t + 1], bias=-8.0)
+            first_pockets()
+        tt(P01, blk(qa, 0), blk(qa, 1), A.max)
+        if t:
+            arrived(t)
+        evicted(t, q2)
+        tt("omv", "mv", OH, A.mult)
         if not last:
-            tool_lists(t + 1)
-            limits(t + 1)
-
-        def reduce(gg):
-            b, q = 6 + gg // 4, gg % 4
-            op("v", lambda: g.vector.tensor_reduce(T.dm[:, gg:gg + 1], T["ps%d" % b][:, 128 * q:128 * q + 128], AxisListType.X, A.min, apply_absolute_value=True),
-               ["ps%d" % b], ["dm%d" % gg], (b,))
-
-        for gg in range(4):
-            reduce(gg)
+            lin(UN, [("idb", "uw"), ("idb", "wf")])
+            act(blk("un", 0), UN)
+        lin(MISS, [("id4m", "ones")], sp=False)
+        for i in range(3):
+            tt(E[i], blk("mall", i), UU, A.is_equal)
+            mm(MISS, "idn8m", E[i], False, i == 2)
+        lin(AUP, [("idb", "omv")] + [("id4m", x) for x in E])
+        tt("ohu", "ohs", UU, A.mult)
+        nexts(0, 128)
+        for h in range(2):
+            pick("ng", DN, h, [("idn", R("an", 128 + 64 * h, 192 + 64 * h))])
         if last:
-            ts("gout", "gsum", 0.5, None, A.mult)
-            out = "gout"
-        wait("g", deps("g", [out], (), ()))
-        g.remote_dma(T["land%d" % t][:, :], T[out][:, :], T.sem["a%d" % t], T.sem.sent, pid, rid, mask)
-        for gg in range(4, 8):
-            reduce(gg)
-        vk, ok_ = "vl%d" % t, "ofl%d" % t
-        dmk = ["dm%d" % q for q in range(8)]
-        op("v", lambda: g.vector.tensor_copy(lst("vl", t), T.ps1[:, 256:264]), ["ps1_2"], [vk], (1,))
-        op("v", lambda: g.vector.tensor_copy(T.vlf[:, :], T.ps1[:, 256:264]), ["ps1_2"], ["vlf"], (1,))
-        op("v", lambda: g.vector.tensor_tensor(T.dup[:, :], T.dm[:, :].indirect(T.kg[:, :]), T.rm[:, :], A.is_equal), dmk + ["kg", "rm"], ["dup"])
-        mm((T.ps2[:, 384:392], "ps2_3", 2), "dup", "rc", True, True)
-        for i in range(2):
-            o = P((4, 2 + i))
-            mm(o, "id8k", "nn", True, False)
-            mm(o, "idh", "uh", False, False)
-            mm(o, ("id4k", "id2k")[i], ("c385", "c769")[i], False, True)
-        tt("s0", "hit", (5, 1), A.is_lt)
-        tt("s1", "hit", (5, 2), A.is_lt)
-        tt("yy", (T.xt[:, 0:W].indirect(lst("vl", t)), "xt"), "shf", A.add, extra=[vk])
-        op("v", lambda: g.vector.tensor_tensor(T.off[:, :], T.vlf[:, :], T.ps2[:, 384:392], A.max), ["vlf", "ps2_3"], ["off"], (2,))
-        tt((0, 0), "q0", (4, 2), A.subtract)
+            ts("h2", q2, 1, -4096, A.logical_shift_right, A.bitwise_and)
+            ts("hv", "qv", 1, -4096, A.logical_shift_right, A.bitwise_and)
+            tt("q2n", "h2", blk("mall", 2), A.add)
+            tt(P01, "hv", "mv", A.add)
+            tt(P01, P01, "q2n", A.subtract)
+            ts("m01", MISS, 0.0, None, A.is_gt)
+            tt("gw", "m01", P01, A.mult)
+            give(t, "gw", "q2n", 1, "land")
+        tt("x1", "ohu", MISS, A.max)
+        tt("vh", "x1", AUP, A.min)
+        tt(DN, "cc", DN, A.mult)
+        tt(blk("un", 1), NH, DN, A.add)
+        if not last:
+            tt("nh", blk("un", 1), OH, A.mult)
+            for r in range(16):
+                mm(top(R(JL, r, 128, 16)), R("nh", r, 128, 16), GROUPS, True, True)
+            act(top("j8"), top(JL))
+            mm(R(JL, 0, 8), top("j8"), top(R("idb", 0, 8)), True, True)
+            tt("g1%d" % t, "qv", MISS, A.min)
+            give(t, "g1%d" % t, q2, 2, blk("qa%d" % (t + 1), 2))
+            cp(lst("jl", t + 1), R(JL, 0, 8))
+            cp(G("tool", jl), blk("un", 0))
+            tool_list(t + 1)
+        lin(OM, [("idb", "ohs")] + [("idn", x) for x in E])
+        act("ohm", OM, RELU)
+        for r in range(16):
+            mm(top(R(VL, r, 128, 16)), R("vh", 8 * r, 8 * r + 8), GROUPS, True, True)
+        cp(top("v8"), top(VL))
+        for b in range(2):
+            bank = "ps%d" % (6 + b)
+            mm(bank, "vh", R("gs", 512 * b, 512 * b + 512), True, False)
+            for q in range(4):
+                mm(blk(bank, q), blk("gsn", 4 * b + q), "vh", False, q == 3)
+        mm(R(VL, 0, 8), top("v8"), top(R("idb", 0, 8)), True, True)
+        mm(R(ZL, 0, 8), top("v8"), top(R("idb", 0, 8)), True, False)
+        for q in range(8):
+            mm(R(SR, 16 * q, 16 * q + 16), "bo", R("ohm", q, 128, 8), True, True)
+        act("shf", SR, IDN, bias=R("rtb", t, t + 1), scale=R("rtn", t, t + 1))
+        tt(R("eq", 0, 512), "ps6", "tri", A.is_equal)
+        tt(R("eq", 512, 1024), "ps7", "tri", A.is_equal)
+        cp(lst("vl", t), R(VL, 0, 8))
+        for q in range(8):
+            mm(R(ZL, q, q + 1), R("eq", q, 1024, 8), R("c4k", 0, 1), False, q == 7)
+        tt("yy", G(XW, lst("vl", t)), "shf", A.add)
+        tt("off", R(ZL, 0, 8), "spare", A.min)
         ts("yc", "yy", 0.0, 255.0, A.max, A.min)
-        op("v", lambda: g.vector.tensor_copy(lst("ofl", t), T.off[:, :]), ["off"], [ok_])
-        tt((0, 1), "q1", (4, 3), A.subtract)
-        op("v", lambda: g.vector.tensor_copy(T.xt[:, :].indirect(lst("ofl", t)), T.yc[:, :]), ["yc", ok_], ["xt"])
-        tt((0, 0), "s0", (0, 0), A.mult)
-        tt((0, 1), "s1", (0, 1), A.mult)
+        cp(lst("ofl", t), "off")
+        cp(G("xt", lst("ofl", t)), "yc")
         if last:
-            dma("y", T.yx[:, :], T.xt[:, 0:W], "ox", r=["xt"])
-            g.scalar.wait_ge(T.sem.a2, nrec)
-            g.scalar.dma_start(T.yp[:, 256:384], T.land2[:, :]).then_inc(T.sem.oq, 16)
+            store("y", T.yx[:, :], XW, "ox")
+        lin(SC, [("idb", "be"), ("idn", "al"), ("id8k", E[0]), ("idn", E[1]), ("idn", E[2])])
+        lin((4, 3), [("idb", "be"), ("idb", "al"), ("id8k", E[1]), ("idn8m", E[0]), ("idn", E[2])])
+        act(blk("ss", 0), SC, SIGN, bias=-0.5)
+        act(blk("ss", 1), (4, 3), SIGN, bias=-1.5)
+        tool = [("idb", "uw"), ("idb", "wf")] * 2 if last else [("idb", blk("un", 0))]
+        new = [[("id8k", ("c50", "c25")[i]), ("id8k", blk("un", 1))] + tool for i in range(2)]
+        if not last:
+            limits(t + 1)
+            for b in range(4):
+                spread(t + 1, b)
+            cp(G("nxt", jl), blk("un", 1))
+            next_list(t + 1)
+            cp(NH, NL)
+            cp(AH, AL)
+        for i in range(2):
+            lin((0, 1 + i), new[i] + [("id4m", blk("ss", i))])
+        if last:
             for i in range(2):
-                tt("q%d" % i, "q%d" % i, (0, i), A.subtract)
+                lin((5, 1 + i), new[i] + [("id4m", "ones"), ("idn4m", blk("ss", i))])
+            tt("qm", blk(qa, 0, 2), blk("mall", 0, 2), A.add)
+            tt("y1", R(NP, 0, 256), "qm", A.max)
+            tt("y2", R(NQ, 0, 256), "y1", A.min)
             for i in range(2):
-                ts("m%d" % i, "q%d" % i, MSK, None, A.bitwise_and)
-            for i in range(2):
-                tt((T.ys[:, 128 * i:128 * i + 128], "ys%d" % i), "q%d" % i, "m%d" % i, A.add)
-            for i in range(2):
-                ts((T.yo[:, 128 * i:128 * i + 128], "yo%d" % i), (T.ys[:, 128 * i:128 * i + 128], "ys%d" % i), 0.5, -1024.0 * (2 - i), A.mult, A.add)
-            dma("s", T.yp[:, 0:256], T.yo[:, :], "op", r=["yo0", "yo1"])
+                act(blk("yo", i), blk("y2", i), IDN, bias=-1024.0 * (2 - i), scale=0.5)
+            store("s", T.yp[:, 0:256], R("yo"), "op")
+            store("s", T.yp[:, 256:384], R("land"), "oq")
+    issue()
     for sem in ("sv", "ss", "sp", "sg"):
         g.wait_ge(T.sem[sem], cnt[sem])
     g.wait_ge(T.sem.sent, NT * len(topo.engines(core, nxt_core)))

@@ -6,37 +6,37 @@ CPY = ActivationFunctionType.Copy
 IDN = ActivationFunctionType.Identity
 RELU = ActivationFunctionType.Relu
 SIGN = ActivationFunctionType.Sign
+SILU = ActivationFunctionType.Silu
 W, MA, J, NT = 1792, 128, 384, 3
-HALF, QUARTER = (("v", 0, 32), ("s", 64, 128), ("v", 32, 64)), (("v", 0, 32), ("s", 32, 64), ("s", 64, 128))
-XV = (HALF, QUARTER, QUARTER)
+WEAR = (("v", 0, 32), ("s", 64, 128), ("v", 32, 64))
 PIECE = 64
+LIFT = 1024.0
 BIG = 4194304.0
-CYCLE, GATHER, SCATTER, LATE, DMA, RATE, FAR = 0.83, 1.1, 2.3, 120, 1500, 450, 5500
 LB = (5, 4, 6, 7)
+CYCLE, GATHER, SCATTER, LATE, DMA, RATE, FAR, HASTE = 1.1, 1.6, 4.0, 150, 1500, 300, 6500, 2
 
 _B, _H, _F, _I, _U = "bfloat16", "float16", "float32", "int32", "uint16"
 SCRATCH = {}
 for _names, _w, _d in (
-        ("sdt", W, _B), ("xt", W + 8 * MA, _B), ("lmt", J, _B), ("rtb", NT, _B), ("rtn", NT, _F), ("nxt", J, _F),
-        ("jtt pkt tool nint mall qa0 qa1 qa2", J, _I), ("jmt kgi", 8, _I), ("jl vl ofl", 8 * NT, _U), ("anl", 256, _U),
-        ("xa sg ov fd ex zer", 2048, _B), ("ng", 2048, _H), ("gm", 144, _B), ("pre pr2 msk land x1 q2n gw", 128, _F),
-        ("lg lgt cc al be ohs ohm shf yy yc m01", 128, _B), ("ee", 384, _B), ("ss", 256, _B), ("an un", 256, _H),
-        ("j8 v8 uw wf nh omv ohu vh", 128, _H), ("qv mv q2c1 q2c2 g10 g11 h2 hv", 128, _I), ("qm y1 y2 yo", 256, _F),
-        ("qt", 256, _I), ("off spare", 8, _F), ("tri", 512, _B), ("k15", 8, _U), ("c4k", 2, _B),
-        ("ones c50 c25 idb idn id8k id4m idn4m idn8m bt bo", 128, _B),
-        ("ep", 160, _B), ("gs gsn eq", 1024, _B)):
+        ("sdt", W, _B), ("xt", W + 8 * MA, _B), ("lmt", J, _B), ("rtb", NT, _B), ("rtn rtf", NT, _F), ("nxt tool", J, _F),
+        ("jtt pkt tint nint mall qa0 qa1 qa2", J, _I), ("jmt kgi", 8, _I), ("jl vl ofl", 8 * NT, _U), ("anl", 256, _U),
+        ("xa sg ov fd ex zer", 2048, _B), ("ng", 2048, _H), ("pre key msk x1 y3 uf nf", 128, _F),
+        ("gm lg lgt cc al be ohs ohm shf yy yc", 128, _B), ("ee", 384, _B), ("ss", 256, _B), ("an un", 256, _H),
+        ("v8 uw wf nh omv ohu vh", 128, _H), ("qv mv q2c1 q2c2 g10 g11 g12 land hi2", 128, _I), ("qm y1 y2 yo", 256, _F),
+        ("qt", 256, _I), ("off spare", 8, _F), ("tri", 512, _B), ("k15", 8, _U), ("c4k", 2, _B), ("e16", 8, _B),
+        ("ones c50 c25 idb idn id8k id4m idn4m idn8m bt bo tie", 128, _B), ("ep", 160, _B), ("gs gsn eq", 1024, _B)):
     for _n in _names.split():
         SCRATCH[_n] = ("sbuf", [128, _w], _d)
 for _k in range(8):
     SCRATCH["ps%d" % _k] = ("psum", [128, 512], _F)
 SEMAPHORES = ["sv", "ss", "sp", "sg", "ljm", "ljt", "llm", "lpk", "lrt", "lxw", "lsd", "a0", "a1", "a2", "sent", "ox", "op", "oq"]
 MSK, NOIDX, NOTAG = 2047, 4188159, 4194303
-P01, NP, DN = (0, 0), (0, 1), (3, 1)
-CNT, MISS, AUP, ZL = (1, 0), (1, 1), (1, 2), (1, 3)
-SUM, OH, JL, VL = (2, 0), (2, 1), (2, 2), (2, 3)
-DU, SR, OM = (3, 0), (3, 2), (3, 3)
-UU, SC = (4, 0), (4, 2)
-UN, NQ = (5, 0), (5, 1)
+P01, NP = (0, 0), (0, 1)
+CNT, VL, MISS, AUP, ZL = (1, 0), (1, 0), (1, 1), (1, 2), (1, 3)
+SUM, OH, SC0, SC1 = (2, 0), (2, 1), (2, 2), (2, 3)
+DU, DN, JL = (3, 0), (3, 1), (3, 2)
+UU = (4, 0)
+UN, OM, NQ, SR, LT = (5, 0), (5, 1), (5, 1), (5, 2), (5, 3)
 
 
 def rank_program(g, core, T, topo):
@@ -111,29 +111,39 @@ def rank_program(g, core, T, topo):
         calls.append(dict(e=e, call=call, busy=busy, late=LATE if late is None else late, token=token, hard=hard, soft=soft - hard - {me}))
         return me
 
-    def issue():
+    def plan(urgency, back):
         succ = [[] for _ in calls]
         left = [0] * len(calls)
         for i, c in enumerate(calls):
             for j in c["hard"] | c["soft"]:
-                succ[j].append(i)
-                left[i] += 1
+                a, b = (i, j) if back else (j, i)
+                succ[a].append((b, calls[j]["late"] if j in c["hard"] else 0))
+                left[b] += 1
         free = {e: 0.0 for e in "vspgyr"}
-        can = [0.0] * len(calls)
-        ready = [i for i in range(len(calls)) if not left[i]]
+        can = [c["late"] if back else 0.0 for c in calls]
+        ready, order, end = [i for i in range(len(calls)) if not left[i]], [], [0.0] * len(calls)
         while ready:
             start = {i: max(can[i], free[calls[i]["e"]]) for i in ready}
-            first = min(ready, key=lambda i: (start[i], i))
-            i = min([first] + [i for i in ready if calls[i]["e"] == calls[first]["e"] and start[i] < start[first] + calls[first]["busy"]])
+            first = min(ready, key=lambda i: (start[i], -urgency[i]))
+            soon = [i for i in ready if calls[i]["e"] == calls[first]["e"] and start[i] < start[first] + calls[first]["busy"]]
+            i = max([first] + soon, key=lambda i: urgency[i] - HASTE * (start[i] - start[first]))
             ready.remove(i)
-            c = calls[i]
-            e = c["e"]
-            free[e] = start[i] + c["busy"]
-            for j in succ[i]:
-                can[j] = max(can[j], free[e] + (c["late"] if i in calls[j]["hard"] else 0))
+            order.append(i)
+            free[calls[i]["e"]] = end[i] = start[i] + calls[i]["busy"]
+            for j, lag in succ[i]:
+                can[j] = max(can[j], end[i] + lag)
                 left[j] -= 1
                 if not left[j]:
                     ready.append(j)
+        return order, end
+
+    def issue():
+        order, end = plan([-1000.0 * i for i in range(len(calls))], False)
+        for rnd in range(3):
+            order, end = plan(plan(end, True)[1], False)
+        for i in order:
+            c = calls[i]
+            e = c["e"]
             known = {}
             if e != "r":
                 wait(e, {calls[j]["token"] for j in c["hard"]})
@@ -147,19 +157,25 @@ def rank_program(g, core, T, topo):
                 known[c["token"][0]] = c["token"][1]
                 snap[c["token"]] = known
 
+    def follow(n):
+        calls[-1]["soft"].update(range(len(calls) - 1 - n, len(calls) - 1))
+
+    def size(x):
+        return 128 * len(x[1][0][1]) * (4 if SCRATCH[x[1][0][0]][2] in (_I, _F) else 2)
+
     def load(e, nm, src, sem, b=None):
         o = R(nm, 0, b)
-        moved[0] += 128 * len(o[1][0][1]) * (4 if SCRATCH[nm][2] == _I else 2)
+        moved[0] += size(o)
         op(e, lambda: ENG[e].dma_start(o[0], src[:, :]).then_inc(T.sem[sem], 16), [o], [], 60, DMA + moved[0] / RATE, (sem, 16))
-        calls[-1]["soft"].update(range(len(calls) - 1))
+        follow(len(calls) - 1)
 
     def store(e, dst, x, sem):
-        op(e, lambda: ENG[e].dma_start(dst, x[0]).then_inc(T.sem[sem], 16), [], [x], 60, DMA, (sem, 16))
+        op(e, lambda: ENG[e].dma_start(dst, x[0]).then_inc(T.sem[sem], 16), [], [x], 60, DMA + size(x) / RATE, (sem, 16))
 
-    def give(t, a, b, fold, dst):
+    def give(t, a, b, dst):
         a, b, dst = R(a), R(b), R(dst)
         move = RemoteDMATransfer(dst_ids=[DstId(rid=rid, pnc=pid)], dma_engine_mask=mask, remote_sem=T.sem["a%d" % t],
-                                 srcs=[a[0], b[0]], dsts=[dst[0]], alu_op=fold)
+                                 srcs=[a[0], b[0]], dsts=[dst[0]], alu_op=2)
         i = op("g", lambda: g.remote_dma_fused([move], local_sem=T.sem.sent), [], [a, b], 100, FAR, False)
         op("r", None, [dst], [], 0, 0, ("a%d" % t, nrec), [i])
 
@@ -195,14 +211,18 @@ def rank_program(g, core, T, topo):
         out, a, b = R(out), R(a), R(b)
         op("v", lambda: g.vector.tensor_tensor_scan(out[0], a[0], b[0], 0.0, A.mult, A.max), [out], [a, b], time(out, [a], 1))
 
-    def act(out, a, func=CPY, bias=0.0, scale=1.0):
+    def act(out, a, func=CPY, bias=0.0, scale=1.0, more=0):
         out, a = R(out), R(a)
-        op("s", lambda: g.scalar.activation(out[0], a[0], func, bias=col(bias), scale=col(scale)), [out], [a] + cols(bias, scale),
-           (75 if len(a) == 2 else 120) + time(out, [a], 1))
+        op("s", lambda: g.scalar.activation(out[0], a[0], func, bias=bias, scale=scale), [out], [a],
+           (75 if len(a) == 2 else 120) + time(out, [a], 1) + more)
+
+    def put(out, a):
+        a = R(a)
+        op("s", lambda: g.scalar.activation(out[0], a[0], SILU), [out], [a], 120 + time(out, [a], 1))
 
     def mm(out, l, r, st, sp):
         out, l, r = R(out), R(l), R(r)
-        op("p", lambda: g.tensor.matmul(out[0], l[0], r[0], st, sp), [out], [l, r], 3 + max(min(64, len(l[1][0][1])), len(r[1][0][1])) * CYCLE / 2)
+        op("p", lambda: g.tensor.matmul(out[0], l[0], r[0], st, sp), [out], [l, r], 3 + max(64, len(r[1][0][1])) * CYCLE / 2)
 
     def lin(out, terms, st=True, sp=True):
         for i, (l, r) in enumerate(terms):
@@ -231,12 +251,12 @@ def rank_program(g, core, T, topo):
     E = [blk("ee", i) for i in range(3)]
     GROUPS = R("bo", 0, 128, 16)
 
-    load("y", "jmt", T.jm, "ljm")
-    load("s", "jtt", T.jt, "ljt")
+    load("s", "jmt", T.jm, "ljm")
+    load("y", "jtt", T.jt, "ljt")
     load("s", "lmt", T.lm, "llm")
     load("y", "xt", T.xw, "lxw", W)
     load("y", "sdt", T.sd, "lsd")
-    load("s", "pkt", T.pk, "lpk")
+    load("y", "pkt", T.pk, "lpk")
     load("y", "rtb", T.rt, "lrt")
 
     fill("ones", 1.0)
@@ -247,6 +267,7 @@ def rank_program(g, core, T, topo):
     fill("zer", 0.0)
     fill("ep", 0.0)
     iota("kgi", [[16, 8]], 15, 0)
+    iota("tie", [[0, 8], [-1, 16]], 15, 0)
     asel("msk", "ones", [[0, 8], [1, 16]], A.is_gt, 0.0, 0, 0)
     asel("gsn", R("zer", 0, 1024), [[16, 8], [0, 128]], A.is_gt, -1.0, 0, -1)
     asel("gsn", "gsn", [[16, 8], [0, 128]], A.is_ge, 0.0, 15, -1)
@@ -254,28 +275,34 @@ def rank_program(g, core, T, topo):
     iota("spare", [[1, 8]], W, 8)
     asel("ex", "zer", [[-1, 128], [0, 16]], A.not_equal, 1.0, 0, 1)
 
+    def consts():
+        for nm, c in (("idn", -1.0), ("id4m", BIG), ("idn8m", -2 * BIG), ("id8k", 8192.0), ("idn4m", -BIG)):
+            ts(nm, "idb", c, None, A.mult)
+        ts("gs", "gsn", -1.0, None, A.mult)
+        ts("rtn", "rtb", -1.0, -8.0, A.mult, A.add)
+        cp("rtf", "rtb")
+        for nm, c in (("c50", 0.5), ("c25", 0.25)):
+            fill(nm, c)
+
     def next_list(t):
-        cp(NL, G("nxt", lst("jl", t)))
+        ts(NL, G("nxt", lst("jl", t)), 0.25 - LIFT, None, A.add)
 
     def tool_list(t):
-        cp(AL, G("tool", lst("jl", t)))
+        ts(AL, G("tool", lst("jl", t)), 0.25 - LIFT, None, A.add)
 
-    def nexts(a, b):
-        for c in range(a, b, PIECE):
-            act(R("ng", 16 * c, 16 * (c + PIECE)), G("nxt", R("anl", 128 + c, 128 + c + PIECE)))
+    def numbers():
+        ts(NH, NL, LIFT, None, A.add)
+        cp(AH, AL)
 
-    def sisters():
+    def long_gather(out, win, first):
         for c in range(0, 128, PIECE):
-            act(R("sg", 16 * c, 16 * (c + PIECE)), G("sdt", R("anl", c, c + PIECE)))
-
-    def wear(e, a, b):
-        e(R("xa", 16 * a, 16 * b), G(XW, R("anl", a, b)))
+            act(R(out, 16 * c, 16 * (c + PIECE)), G(win, R("anl", first + c, first + c + PIECE)))
 
     def limits(t):
         act("lg", G("lmt", lst("jl", t)))
         if t:
-            mm(OM, "lg", "idb", True, True)
-            act("lgt", OM)
+            mm(LT, "lg", "idb", True, True)
+            act("lgt", LT)
 
     def spread(t, b):
         if t:
@@ -292,14 +319,6 @@ def rank_program(g, core, T, topo):
     def pick(src, piece, h, first):
         o = R(piece, 64 * h, 64 * h + 64)
         lin(o, first + [(blk("fd", k), R(src, 1024 * h + k, 1024 * h + 1024, 16)) for k in range(16)])
-
-    def consts():
-        for nm, c in (("idn", -1.0), ("id4m", BIG), ("idn8m", -2 * BIG), ("id8k", 8192.0), ("idn4m", -BIG)):
-            ts(nm, "idb", c, None, A.mult)
-        ts("gs", "gsn", -1.0, None, A.mult)
-        ts("rtn", "rtb", -1.0, -8.0, A.mult, A.add)
-        for nm, c in (("c50", 0.5), ("c25", 0.25), ("c4k", 4096.0)):
-            fill(nm, c)
 
     def first_pockets():
         ts("mall", "pkt", 4095, None, A.bitwise_and)
@@ -324,12 +343,15 @@ def rank_program(g, core, T, topo):
         tt("be", P01, q2, A.is_gt)
 
     cp(lst("jl", 0), "jmt")
-    ts("tool", "jtt", 4095, None, A.bitwise_and)
+    ts("tint", "jtt", 4095, None, A.bitwise_and)
+    ts("tool", "tint", LIFT, None, A.add)
     tool_list(0)
+    act("c4k", R("ones", 0, 2), SILU, scale=4096.0, more=1300)
     limits(0)
+    follow(1)
     cp(R("ep", 16, 144, 16), GROUPS)
     cp("k15", "kgi")
-    fill(R("gm", 0, 16), 1.0)
+    ts("e16", GROUPS, 16.0, None, A.mult)
     for b in range(4):
         spread(0, b)
     for k in range(16):
@@ -339,36 +361,38 @@ def rank_program(g, core, T, topo):
         last = t == NT - 1
         jl, qa = lst("jl", t), "qa%d" % t
         q2 = R("q2c%d" % t) if t else blk(qa, 2)
-        for e, a, b in XV[t]:
-            wear(cp if e == "v" else act, a, b)
+        for e, a, b in WEAR:
+            (cp if e == "v" else act)(R("xa", 16 * a, 16 * b), G(XW, R("anl", a, b)))
         if t == 0:
             ts("nint", "jtt", 12, None, A.logical_shift_right)
-            cp("nxt", "nint")
+            ts("nxt", "nint", LIFT, None, A.add)
             next_list(0)
-            cp("an", "anl")
+            numbers()
         compare(0)
         compare(1)
         count(0)
         compare(2)
         compare(3)
         count(1)
+        mm(SUM, "idb", "tie", True, False)
         for k in range(16):
-            mm(R(SUM, k, 128, 16), R("xa", k, 2048, 16), GROUPS, True, True)
+            mm(R(SUM, k, 128, 16), R("xa", k, 2048, 16), "e16", False, k == 15)
         ts("cc", CNT, 9.0, None, A.is_ge)
-        sisters()
+        long_gather("sg", "sdt", 0)
         pick("sg", DU, 0, [])
         pick("sg", DU, 1, [])
         tt(DU, "cc", DU, A.mult)
         tt("uw", AH, DU, A.add)
         ts("wf", "uw", float(W), -float(W), A.is_ge, A.mult)
         lin(UU, [("idb", "uw"), ("idb", "wf")])
-        for pre in ("pre", "pr2"):
-            scan(pre, "msk", SUM)
-        tt(R("gm", 16, 144), G("pre", "k15"), "pr2", A.is_equal)
+        scan("pre", "msk", SUM)
+        cp("key", SUM)
+        tt("gm", G("pre", "k15"), "key", A.is_equal)
         if t == 0:
             consts()
-        lin(OH, [(R("gm", 16, 144), "idb"), (R("gm", 15, 143), "idn"), (blk("fd", 0), "ones")])
-        act("ohs", OH)
+        mm(OH, "gm", "idb", True, True)
+        mm(LT, "gm", "idb", True, True)
+        act("ohs", LT)
         if t:
             update(t - 1)
         else:
@@ -378,41 +402,36 @@ def rank_program(g, core, T, topo):
             arrived(t)
         evicted(t, q2)
         tt("omv", "mv", OH, A.mult)
-        if not last:
-            lin(UN, [("idb", "uw"), ("idb", "wf")])
-            act(blk("un", 0), UN)
+        lin(UN, [("idb", "uw"), ("idb", "wf")])
+        if last:
+            act(blk("un", 0), UN, scale=2.0)
+        else:
+            act("uf", UN, IDN, bias=LIFT)
         lin(MISS, [("id4m", "ones")], sp=False)
         for i in range(3):
             tt(E[i], blk("mall", i), UU, A.is_equal)
             mm(MISS, "idn8m", E[i], False, i == 2)
         lin(AUP, [("idb", "omv")] + [("id4m", x) for x in E])
         tt("ohu", "ohs", UU, A.mult)
-        nexts(0, 128)
+        long_gather("ng", "nxt", 128)
         for h in range(2):
             pick("ng", DN, h, [("idn", R("an", 128 + 64 * h, 192 + 64 * h))])
         if last:
-            ts("h2", q2, 1, -4096, A.logical_shift_right, A.bitwise_and)
-            ts("hv", "qv", 1, -4096, A.logical_shift_right, A.bitwise_and)
-            tt("q2n", "h2", blk("mall", 2), A.add)
-            tt(P01, "hv", "mv", A.add)
-            tt(P01, P01, "q2n", A.subtract)
-            ts("m01", MISS, 0.0, None, A.is_gt)
-            tt("gw", "m01", P01, A.mult)
-            give(t, "gw", "q2n", 1, "land")
+            tt("g12", "qv", MISS, A.min)
+            give(t, "g12", q2, "land")
         tt("x1", "ohu", MISS, A.max)
         tt("vh", "x1", AUP, A.min)
         tt(DN, "cc", DN, A.mult)
-        tt(blk("un", 1), NH, DN, A.add)
+        tt(blk("un", 1) if last else "nf", NH, DN, A.add)
         if not last:
-            tt("nh", blk("un", 1), OH, A.mult)
-            for r in range(16):
-                mm(top(R(JL, r, 128, 16)), R("nh", r, 128, 16), GROUPS, True, True)
-            act(top("j8"), top(JL))
-            mm(R(JL, 0, 8), top("j8"), top(R("idb", 0, 8)), True, True)
+            tt("nh", "nf", OH, A.mult)
+            lin(R(JL, 0, 8), [(R("ep", 16 - r, 144 - r), R("nh", r, 128, 16)) for r in range(16)])
             tt("g1%d" % t, "qv", MISS, A.min)
-            give(t, "g1%d" % t, q2, 2, blk("qa%d" % (t + 1), 2))
-            cp(lst("jl", t + 1), R(JL, 0, 8))
-            cp(G("tool", jl), blk("un", 0))
+            give(t, "g1%d" % t, q2, blk("qa%d" % (t + 1), 2))
+            ts(lst("jl", t + 1), R(JL, 0, 8), -LIFT, None, A.add)
+            put(G("tool", jl), "uf")
+            put(G("nxt", jl), "nf")
+            act(blk("un", 1), "nf")
             tool_list(t + 1)
         lin(OM, [("idb", "ohs")] + [("idn", x) for x in E])
         act("ohm", OM, RELU)
@@ -428,7 +447,7 @@ def rank_program(g, core, T, topo):
         mm(R(ZL, 0, 8), top("v8"), top(R("idb", 0, 8)), True, False)
         for q in range(8):
             mm(R(SR, 16 * q, 16 * q + 16), "bo", R("ohm", q, 128, 8), True, True)
-        act("shf", SR, IDN, bias=R("rtb", t, t + 1), scale=R("rtn", t, t + 1))
+        ts("shf", SR, R("rtn", t, t + 1), R("rtf", t, t + 1), A.mult, A.add)
         tt(R("eq", 0, 512), "ps6", "tri", A.is_equal)
         tt(R("eq", 512, 1024), "ps7", "tri", A.is_equal)
         cp(lst("vl", t), R(VL, 0, 8))
@@ -441,20 +460,17 @@ def rank_program(g, core, T, topo):
         cp(G("xt", lst("ofl", t)), "yc")
         if last:
             store("y", T.yx[:, :], XW, "ox")
-        lin(SC, [("idb", "be"), ("idn", "al"), ("id8k", E[0]), ("idn", E[1]), ("idn", E[2])])
-        lin((4, 3), [("idb", "be"), ("idb", "al"), ("id8k", E[1]), ("idn8m", E[0]), ("idn", E[2])])
-        act(blk("ss", 0), SC, SIGN, bias=-0.5)
-        act(blk("ss", 1), (4, 3), SIGN, bias=-1.5)
-        tool = [("idb", "uw"), ("idb", "wf")] * 2 if last else [("idb", blk("un", 0))]
-        new = [[("id8k", ("c50", "c25")[i]), ("id8k", blk("un", 1))] + tool for i in range(2)]
+        lin(SC0, [("idb", "be"), ("idn", "al"), ("id8k", E[0]), ("idn", E[1]), ("idn", E[2])])
+        lin(SC1, [("idb", "be"), ("idb", "al"), ("idn", "ones"), ("id8k", E[1]), ("idn8m", E[0]), ("idn", E[2])])
+        act("ss", R(SC0, 0, 256), SIGN, bias=-0.5)
+        tool = [("idb", blk("un", 0))] if last else [("idb", "uw"), ("idb", "wf")]
+        new = [[("id8k", ("c50", "c25")[i]), ("id8k", blk("un", 1)), ("idn8m", "ones")] + tool for i in range(2)]
         if not last:
             limits(t + 1)
             for b in range(4):
                 spread(t + 1, b)
-            cp(G("nxt", jl), blk("un", 1))
             next_list(t + 1)
-            cp(NH, NL)
-            cp(AH, AL)
+            numbers()
         for i in range(2):
             lin((0, 1 + i), new[i] + [("id4m", blk("ss", i))])
         if last:
@@ -466,7 +482,10 @@ def rank_program(g, core, T, topo):
             for i in range(2):
                 act(blk("yo", i), blk("y2", i), IDN, bias=-1024.0 * (2 - i), scale=0.5)
             store("s", T.yp[:, 0:256], R("yo"), "op")
-            store("s", T.yp[:, 256:384], R("land"), "oq")
+            ts("hi2", "land", 1, -4096, A.logical_shift_right, A.bitwise_and)
+            ts("mv", "land", MSK, None, A.bitwise_and)
+            tt("y3", "hi2", "mv", A.add)
+            store("s", T.yp[:, 256:384], R("y3"), "oq")
     issue()
     for sem in ("sv", "ss", "sp", "sg"):
         g.wait_ge(T.sem[sem], cnt[sem])

@@ -8,23 +8,31 @@ RELU = ActivationFunctionType.Relu
 SIGN = ActivationFunctionType.Sign
 SILU = ActivationFunctionType.Silu
 W, MA, J, NT = 1792, 128, 384, 3
-WEAR = (("v", 0, 32), ("s", 64, 128), ("v", 32, 64))
-PIECE = 64
+WEAR = [(("v", 0, 64), ("v", 64, 128)),
+        (("v", 0, 64), ("s", 64, 128)),
+        (("v", 0, 32), ("s", 48, 96), ("v", 32, 48), ("s", 96, 128))]
+EARLY = [128, 0, 0]
+SOON = [0, 128, 128]
 LIFT = 1024.0
 BIG = 4194304.0
 LB = (5, 4, 6, 7)
-CYCLE, GATHER, SCATTER, LATE, DMA, RATE, FAR, HASTE = 1.1, 1.6, 4.0, 150, 1500, 300, 6500, 2
+CYCLE, GATHER, SCATTER, LATE, DMA, RATE, FAR, FIRST = 0.85, 1.35, 2.6, 140, 1500, 400, 3500, 5500
+CALL = {"v": (10, 50), "s": (75, 100), "g": (150, 0)}
+PIPE = 150
+ROUNDS = 6
+ORDER = []
+OPT = dict(key="vvv", ohu="vvv", nh="vv", ids=5, sc=0, cmp="qqq", fin=1, un=1, ex=0, sis="sps", cuts={}, nw=1, nfirst="aa", lgat=64, chain="", loads="yjt yxw ylm ysd ypk yrt")
 
 _B, _H, _F, _I, _U = "bfloat16", "float16", "float32", "int32", "uint16"
 SCRATCH = {}
 for _names, _w, _d in (
-        ("sdt", W, _B), ("xt", W + 8 * MA, _B), ("lmt", J, _B), ("rtb", NT, _B), ("rtn rtf", NT, _F), ("nxt tool", J, _F),
-        ("jtt pkt tint nint mall qa0 qa1 qa2", J, _I), ("jmt kgi", 8, _I), ("jl vl ofl", 8 * NT, _U), ("anl", 256, _U),
-        ("xa sg ov fd ex zer", 2048, _B), ("ng", 2048, _H), ("pre key msk x1 y3 uf nf", 128, _F),
-        ("gm lg lgt cc al be ohs ohm shf yy yc", 128, _B), ("ee", 384, _B), ("ss", 256, _B), ("an un", 256, _H),
-        ("v8 uw wf nh omv ohu vh", 128, _H), ("qv mv q2c1 q2c2 g10 g11 g12 land hi2", 128, _I), ("qm y1 y2 yo", 256, _F),
-        ("qt", 256, _I), ("off spare", 8, _F), ("tri", 512, _B), ("k15", 8, _U), ("c4k", 2, _B), ("e16", 8, _B),
-        ("ones c50 c25 idb idn id8k id4m idn4m idn8m bt bo tie", 128, _B), ("ep", 160, _B), ("gs gsn eq", 1024, _B)):
+        ("sdt", W, _B), ("xt", W + 8 * MA, _B), ("lmt", J, _B), ("rtb", NT, _B), ("rtn", NT, _F), ("nxt tool", J, _F),
+        ("jtt pkt tint mall qa0 qa1 qa2", J, _I), ("jmt kgi", 8, _I), ("jl vl ofl", 8 * NT, _U), ("anl", 256, _U),
+        ("xa sg ov ex", 2048, _B), ("ng", 2048, _H), ("pre key msk y3 uf nf rs js vs os_", 128, _F),
+        ("gm lg lgt cc al be wf shf yy yc", 128, _B), ("ee", 384, _B), ("ss tags ends", 256, _B), ("an", 512, _H), ("un", 256, _H),
+        ("sis cd cn nh omv ohu x1 vh", 128, _H), ("qv mv q2c1 q2c2 g10 g11 g12 land hi2", 128, _I), ("y1 yo", 256, _F),
+        ("qt", 256, _I), ("zer", 512, _B), ("tri", 256, _B), ("k15", 8, _U), ("cb", 240, _B),
+        ("ones cn15 idb idn idw id2k id8k id4m idn4k idn1m idn8m bt bo tie sel dm", 128, _B), ("gs gsn eq", 1024, _B)):
     for _n in _names.split():
         SCRATCH[_n] = ("sbuf", [128, _w], _d)
 for _k in range(8):
@@ -32,11 +40,14 @@ for _k in range(8):
 SEMAPHORES = ["sv", "ss", "sp", "sg", "ljm", "ljt", "llm", "lpk", "lrt", "lxw", "lsd", "a0", "a1", "a2", "sent", "ox", "op", "oq"]
 MSK, NOIDX, NOTAG = 2047, 4188159, 4194303
 P01, NP = (0, 0), (0, 1)
-CNT, VL, MISS, AUP, ZL = (1, 0), (1, 0), (1, 1), (1, 2), (1, 3)
-SUM, OH, SC0, SC1 = (2, 0), (2, 1), (2, 2), (2, 3)
-DU, DN, JL = (3, 0), (3, 1), (3, 2)
-UU = (4, 0)
-UN, OM, NQ, SR, LT = (5, 0), (5, 1), (5, 1), (5, 2), (5, 3)
+CNT, VL, UH, OH, ZL = (1, 0), (1, 0), (1, 1), (1, 2), (1, 3)
+SUM, UN, NN = (2, 0), (2, 2), (2, 3)
+DU, SIS, LT, SR = (3, 0), (3, 1), (3, 3), (3, 2)
+UU, SC = (4, 0), (4, 0)
+DN, NQ = (5, 0), (5, 1)
+MARK = (6, 0)
+AUP, LIM = (7, 0), (7, 1)
+DIF = ((7, 0), (6, 0), (4, 0), (7, 2))
 
 
 def rank_program(g, core, T, topo):
@@ -55,22 +66,18 @@ def rank_program(g, core, T, topo):
     clk = {e: {} for e in ENG}
     snap = {}
     calls = []
-    used, turn = {}, {}
     moved = [0]
+    chain, before = set(), {}
+    used, turn = {}, {}
 
-    def R(x, a=0, b=None, step=1):
+    def R(x, a=0, b=None, step=1, rows=128):
         if isinstance(x, str):
             b = SCRATCH[x][1][1] if b is None else b
-            return T[x][:, a:b:step], [(x, frozenset(range(a, b, step)))]
+            return T[x][0:rows, a:b:step], [(x, frozenset(range(a, b, step)))]
         if isinstance(x[0], int):
             base = 128 * x[1]
             return R("ps%d" % x[0], base + a, base + (128 if b is None else b), step)
         return x
-
-    def top(x):
-        nm, c = R(x)[1][0]
-        c = sorted(c)
-        return T[nm][0:8, c[0]:c[-1] + 1:c[1] - c[0]], [(nm, frozenset(c))]
 
     def G(win, off):
         win, off = R(win), R(off)
@@ -88,7 +95,19 @@ def rank_program(g, core, T, topo):
                 if clk[e].get(a, 0) < b:
                     clk[e][a] = b
 
-    def op(e, call, outs, ins, busy, late=None, token=None, after=()):
+    def span(e, outs, ins, per):
+        n = len(outs[0][1][0][1])
+        if e == "p":
+            return 3 + max(64, n) * CYCLE / 2
+        if len(outs[0]) > 2:
+            return CALL[e][1] + 16 * len(outs[0][2][0][1]) * SCATTER
+        if ins and len(ins[0]) > 2:
+            return CALL[e][1] + n * GATHER
+        if per is None:
+            per = 0.5 if e == "v" and all(SCRATCH[x[1][0][0]][2] in (_B, _H, _U) for x in outs + ins[:1]) else 1
+        return CALL[e][0] + max(64, n * per) * CYCLE
+
+    def op(e, call, outs, ins, token=None, late=None, after=(), per=None, more=0):
         acc = []
         for o in outs:
             acc += [(nm, c, True) for nm, c in o[1]] + [(nm, c, False) for x in o[2:] for nm, c in x]
@@ -108,57 +127,63 @@ def rank_program(g, core, T, topo):
                     same = calls[i]["e"] == e and token is None and calls[i]["token"] is None
                     (soft if same and (e == "p" or not wrt2) else hard).add(i)
             used[nm] = [u for u in old if not (wrt and u[1] <= c)] + [(me, c, wrt)]
-        calls.append(dict(e=e, call=call, busy=busy, late=LATE if late is None else late, token=token, hard=hard, soft=soft - hard - {me}))
+        if e in chain:
+            soft.update(i for i in range(me) if calls[i]["e"] == e and i >= before.get(e, 0))
+            before[e] = me
+        busy = more + (span(e, outs, ins, per) if token is None else 60 if call else 0)
+        calls.append(dict(e=e, call=call, busy=busy, late=LATE + (PIPE if e == "p" else 0) if late is None else late, token=token, hard=hard, soft=soft - hard - {me}))
         return me
 
-    def plan(urgency, back):
-        succ = [[] for _ in calls]
-        left = [0] * len(calls)
+    def place(order, back):
+        need = [[] for _ in calls]
         for i, c in enumerate(calls):
             for j in c["hard"] | c["soft"]:
                 a, b = (i, j) if back else (j, i)
-                succ[a].append((b, calls[j]["late"] if j in c["hard"] else 0))
-                left[b] += 1
-        free = {e: 0.0 for e in "vspgyr"}
-        can = [c["late"] if back else 0.0 for c in calls]
-        ready, order, end = [i for i in range(len(calls)) if not left[i]], [], [0.0] * len(calls)
-        while ready:
-            start = {i: max(can[i], free[calls[i]["e"]]) for i in ready}
-            first = min(ready, key=lambda i: (start[i], -urgency[i]))
-            soon = [i for i in ready if calls[i]["e"] == calls[first]["e"] and start[i] < start[first] + calls[first]["busy"]]
-            i = max([first] + soon, key=lambda i: urgency[i] - HASTE * (start[i] - start[first]))
-            ready.remove(i)
-            order.append(i)
-            free[calls[i]["e"]] = end[i] = start[i] + calls[i]["busy"]
-            for j, lag in succ[i]:
-                can[j] = max(can[j], end[i] + lag)
-                left[j] -= 1
-                if not left[j]:
-                    ready.append(j)
-        return order, end
+                need[b].append((a, calls[j]["late"] if j in c["hard"] else 0))
+        taken, end = {e: [] for e in "vspgyr"}, [None] * len(calls)
+
+        def fit(i):
+            for j, lag in need[i]:
+                if end[j] is None:
+                    fit(j)
+            at, busy = max([end[j] + lag for j, lag in need[i]] + [calls[i]["late"] if back else 0]), calls[i]["busy"]
+            line = taken[calls[i]["e"]]
+            k = 0
+            while k < len(line) and line[k][0] < at + busy:
+                at, k = max(at, line[k][1]), k + 1
+            line.insert(k, (at, at + busy))
+            end[i] = at + busy
+
+        for i in order:
+            if end[i] is None:
+                fit(i)
+        return end
 
     def issue():
-        order, end = plan([-1000.0 * i for i in range(len(calls))], False)
-        for rnd in range(3):
-            order, end = plan(plan(end, True)[1], False)
-        for i in order:
+        every = range(len(calls))
+        if not ORDER:
+            end, best = place(every, False), None
+            for rnd in range(ROUNDS):
+                end = place(sorted(every, key=lambda i: (-end[i], -i)), True)
+                end = place(sorted(every, key=lambda i: (-end[i], i)), False)
+                total = max(end[i] + calls[i]["late"] for i in every)
+                if best is None or total < best:
+                    best, ORDER[:] = total, sorted(every, key=lambda i: (end[i] - calls[i]["busy"], end[i], i))
+        for i in ORDER:
             c = calls[i]
             e = c["e"]
             known = {}
             if e != "r":
                 wait(e, {calls[j]["token"] for j in c["hard"]})
-                ins = c["call"]()
+                done = c["call"]()
                 if c["token"] is None:
                     cnt[OWN[e]] += 1
                     c["token"] = (OWN[e], cnt[OWN[e]])
-                    ins.then_inc(T.sem[OWN[e]], 1)
+                    done.then_inc(T.sem[OWN[e]], 1)
                 known = dict(clk[e])
             if c["token"]:
                 known[c["token"][0]] = c["token"][1]
                 snap[c["token"]] = known
-
-    def follow(n):
-        calls[-1]["soft"].update(range(len(calls) - 1 - n, len(calls) - 1))
 
     def size(x):
         return 128 * len(x[1][0][1]) * (4 if SCRATCH[x[1][0][0]][2] in (_I, _F) else 2)
@@ -166,27 +191,18 @@ def rank_program(g, core, T, topo):
     def load(e, nm, src, sem, b=None):
         o = R(nm, 0, b)
         moved[0] += size(o)
-        op(e, lambda: ENG[e].dma_start(o[0], src[:, :]).then_inc(T.sem[sem], 16), [o], [], 60, DMA + moved[0] / RATE, (sem, 16))
-        follow(len(calls) - 1)
+        i = op(e, lambda: ENG[e].dma_start(o[0], src[:, :]).then_inc(T.sem[sem], 16), [o], [], (sem, 16), DMA + moved[0] / RATE)
+        calls[i]["soft"].update(range(i))
 
     def store(e, dst, x, sem):
-        op(e, lambda: ENG[e].dma_start(dst, x[0]).then_inc(T.sem[sem], 16), [], [x], 60, DMA + size(x) / RATE, (sem, 16))
+        op(e, lambda: ENG[e].dma_start(dst, x[0]).then_inc(T.sem[sem], 16), [], [x], (sem, 16), DMA + size(x) / RATE)
 
     def give(t, a, b, dst):
         a, b, dst = R(a), R(b), R(dst)
         move = RemoteDMATransfer(dst_ids=[DstId(rid=rid, pnc=pid)], dma_engine_mask=mask, remote_sem=T.sem["a%d" % t],
                                  srcs=[a[0], b[0]], dsts=[dst[0]], alu_op=2)
-        i = op("g", lambda: g.remote_dma_fused([move], local_sem=T.sem.sent), [], [a, b], 100, FAR, False)
-        op("r", None, [dst], [], 0, 0, ("a%d" % t, nrec), [i])
-
-    def time(out, ins, per):
-        n = len(out[1][0][1]) if len(out) == 2 else 16 * len(out[2][0][1])
-        if len(out) > 2:
-            return 60 + n * SCATTER
-        return 60 + n * GATHER if len(ins[0]) > 2 else 10 + max(64, n * per) * CYCLE
-
-    def short(*xs):
-        return 0.5 if all(SCRATCH[x[1][0][0]][2] in (_B, _H, _U) for x in xs) else 1
+        i = op("g", lambda: g.remote_dma_fused([move], local_sem=T.sem.sent), [], [a, b], False, FAR, more=0 if t else FIRST)
+        op("r", None, [dst], [], ("a%d" % t, nrec), LATE, [i])
 
     def col(x):
         return x[0] if isinstance(x, tuple) else x
@@ -197,32 +213,39 @@ def rank_program(g, core, T, topo):
     def tt(out, a, b, o):
         out, a, b = R(out), R(a), R(b)
         both = SCRATCH[a[1][0][0]][0] == SCRATCH[b[1][0][0]][0]
-        op("v", lambda: g.vector.tensor_tensor(out[0], a[0], b[0], o), [out], [a, b], time(out, [a], 1 + both))
+        op("v", lambda: g.vector.tensor_tensor(out[0], a[0], b[0], o), [out], [a, b], per=1 + both)
 
     def ts(out, a, s1, s2, *o):
         out, a = R(out), R(a)
-        op("v", lambda: g.vector.tensor_scalar(out[0], a[0], col(s1), col(s2), *o), [out], [a] + cols(s1, s2), time(out, [a], short(out, a)))
+        op("v", lambda: g.vector.tensor_scalar(out[0], a[0], col(s1), col(s2), *o), [out], [a] + cols(s1, s2))
 
-    def cp(out, a):
+    def cp(out, a, e="v"):
+        if e == "s":
+            return act(out, a)
         out, a = R(out), R(a)
-        op("v", lambda: g.vector.tensor_copy(out[0], a[0]), [out], [a], time(out, [a], short(out, a)))
+        op("v", lambda: g.vector.tensor_copy(out[0], a[0]), [out], [a])
 
-    def scan(out, a, b):
+    def scan(out, a, b, o0, o1):
         out, a, b = R(out), R(a), R(b)
-        op("v", lambda: g.vector.tensor_tensor_scan(out[0], a[0], b[0], 0.0, A.mult, A.max), [out], [a, b], time(out, [a], 1))
+        op("v", lambda: g.vector.tensor_tensor_scan(out[0], a[0], b[0], 0.0, o0, o1), [out], [a, b])
 
-    def act(out, a, func=CPY, bias=0.0, scale=1.0, more=0):
+    def act(out, a, func=CPY, bias=0.0, scale=1.0):
         out, a = R(out), R(a)
-        op("s", lambda: g.scalar.activation(out[0], a[0], func, bias=bias, scale=scale), [out], [a],
-           (75 if len(a) == 2 else 120) + time(out, [a], 1) + more)
+        op("s", lambda: g.scalar.activation(out[0], a[0], func, bias=bias, scale=scale), [out], [a], more=1300 if func is SILU else 0)
 
     def put(out, a):
         a = R(a)
-        op("s", lambda: g.scalar.activation(out[0], a[0], SILU), [out], [a], 120 + time(out, [a], 1))
+        op("s", lambda: g.scalar.activation(out[0], a[0], SILU), [out], [a])
+
+    def above(e, out, a, c):
+        if e == "v":
+            ts(out, a, -c, 0.0, A.add, A.max)
+        else:
+            act(out, a, RELU, bias=-c)
 
     def mm(out, l, r, st, sp):
         out, l, r = R(out), R(l), R(r)
-        op("p", lambda: g.tensor.matmul(out[0], l[0], r[0], st, sp), [out], [l, r], 3 + max(64, len(r[1][0][1])) * CYCLE / 2)
+        op("p", lambda: g.tensor.matmul(out[0], l[0], r[0], st, sp), [out], [l, r])
 
     def lin(out, terms, st=True, sp=True):
         for i, (l, r) in enumerate(terms):
@@ -230,15 +253,15 @@ def rank_program(g, core, T, topo):
 
     def fill(x, c):
         x = R(x)
-        op("v", lambda: g.vector.memset(x[0], c), [x], [], time(x, [x], short(x)))
+        op("v", lambda: g.vector.memset(x[0], c), [x], [])
 
     def asel(out, in_, pat, cmp_, f, base, cm):
         out, in_ = R(out), R(in_)
-        op("g", lambda: g.affine_select(out[0], in_[0], pat, cmp_, f, base, cm), [out], [in_], 150 + time(out, [in_], 2))
+        op("g", lambda: g.affine_select(out[0], in_[0], pat, cmp_, f, base, cm), [out], [in_], per=2)
 
     def iota(out, pat, base, cm):
         o = R(out)
-        op("g", lambda: g.iota(o[0], pat, base, cm, allow_small_or_imprecise_dtypes=SCRATCH[out][2] != _I), [o], [], 150)
+        op("g", lambda: g.iota(o[0], pat, base, cm, allow_small_or_imprecise_dtypes=SCRATCH[o[1][0][0]][2] != _I), [o], [], per=2)
 
     def blk(x, i, n=1):
         return R(x, 128 * i, 128 * (i + n))
@@ -247,42 +270,54 @@ def rank_program(g, core, T, topo):
         return R(nm, 8 * t, 8 * t + 8)
 
     XW = R("xt", 0, W)
-    AL, NL, AH, NH = blk("anl", 0), blk("anl", 1), blk("an", 0), blk("an", 1)
+    AL, NL = blk("anl", 0), blk("anl", 1)
     E = [blk("ee", i) for i in range(3)]
     GROUPS = R("bo", 0, 128, 16)
+    TWO = R("ones", rows=2)
+
+    def firsts(t):
+        return blk("an", 2 * (t % 2))
+
+    def nexts(t):
+        return blk("an", 2 * (t % 2) + 1)
 
     load("s", "jmt", T.jm, "ljm")
-    load("y", "jtt", T.jt, "ljt")
-    load("s", "lmt", T.lm, "llm")
-    load("y", "xt", T.xw, "lxw", W)
-    load("y", "sdt", T.sd, "lsd")
-    load("y", "pkt", T.pk, "lpk")
-    load("y", "rtb", T.rt, "lrt")
+    for nm in OPT["loads"].split():
+        load(nm[0], {"rt": "rtb", "xw": "xt"}.get(nm[1:], nm[1:] + "t"), T[nm[1:]], "l" + nm[1:], W if nm[1:] == "xw" else None)
 
-    fill("ones", 1.0)
-    asel("idb", "ones", [[-1, 128]], A.is_equal, 0.0, 0, 1)
-    asel("bt", "ones", [[-16, 8], [0, 16]], A.is_ge, 0.0, 0, 1)
-    asel("bo", "bt", [[16, 8], [0, 16]], A.is_ge, 0.0, 15, -1)
-    fill("fd", 0.0)
     fill("zer", 0.0)
-    fill("ep", 0.0)
+    fill("ones", 1.0)
+    fill("cb", 0.0)
     iota("kgi", [[16, 8]], 15, 0)
+    asel("bt", blk("zer", 0), [[16, 8], [0, 16]], A.is_gt, 16.0, 0, -1)
+    asel("bo", "bt", [[16, 8], [0, 16]], A.is_ge, 0.0, 15, -1)
+    asel("idb", "ones", [[-1, 128]], A.is_equal, 0.0, 0, 1)
     iota("tie", [[0, 8], [-1, 16]], 15, 0)
     asel("msk", "ones", [[0, 8], [1, 16]], A.is_gt, 0.0, 0, 0)
-    asel("gsn", R("zer", 0, 1024), [[16, 8], [0, 128]], A.is_gt, -1.0, 0, -1)
-    asel("gsn", "gsn", [[16, 8], [0, 128]], A.is_ge, 0.0, 15, -1)
-    asel("tri", R("zer", 0, 512), [[0, 4], [1, 128]], A.is_gt, 0.5, 0, -1)
-    iota("spare", [[1, 8]], W, 8)
-    asel("ex", "zer", [[-1, 128], [0, 16]], A.not_equal, 1.0, 0, 1)
-
-    def consts():
-        for nm, c in (("idn", -1.0), ("id4m", BIG), ("idn8m", -2 * BIG), ("id8k", 8192.0), ("idn4m", -BIG)):
-            ts(nm, "idb", c, None, A.mult)
-        ts("gs", "gsn", -1.0, None, A.mult)
-        ts("rtn", "rtb", -1.0, -8.0, A.mult, A.add)
-        cp("rtf", "rtb")
-        for nm, c in (("c50", 0.5), ("c25", 0.25)):
-            fill(nm, c)
+    asel("sel", "ones", [[0, 8], [1, 16]], A.is_equal, 0.0, 0, -1)
+    act(R("cb", 112, 128), R("ones", 0, 16), SILU, scale=65536.0)
+    for i, (nm, c) in enumerate((("idn", -1.0), ("idw", -W / 2), ("id2k", 2048.0), ("id8k", 8192.0), ("idn8m", -2 * BIG), ("id4m", BIG),
+                                 ("idn4k", -4096.0), ("idn1m", -BIG / 4))):
+        if i < OPT["ids"]:
+            act(nm, "idb", scale=c)
+        else:
+            asel(nm, blk("zer", 0), [[-1, 128]], A.not_equal, c, 0, 1)
+    mm(P01, "sel", "sel", True, True)
+    act("dm", P01, IDN, BIG, -BIG)
+    iota("cn15", [[0, 128]], -15, 0)
+    iota("rs", [[16, 8], [0, 16]], 16 * W, 128)
+    asel("rs", "rs", [[0, 8], [1, 16]], A.is_equal, 0.0, 0, 0)
+    for b in range(2):
+        half = R("gsn", 512 * b, 512 * b + 512)
+        asel(half, "zer", [[16, 4], [0, 128]], A.is_gt, -1.0, 64 * b, -1)
+        asel(half, half, [[16, 4], [0, 128]], A.is_ge, 0.0, 64 * b + 15, -1)
+    asel("tri", blk("zer", 0, 2), [[0, 2], [1, 128]], A.is_gt, 0.5, 0, -1)
+    for i in range(2):
+        tag = 2048 * (2 - i)
+        iota(R("tags", 128 * i, 128 * i + 128, rows=2), [[0, 128]], -2 * int(BIG), 2 * int(BIG) + tag)
+        iota(R("ends", 128 * i, 128 * i + 128, rows=2), [[0, 128]], 3 * int(BIG) // 4, -3 * int(BIG) // 4 - tag)
+    for b in range(4 if OPT["ex"] else 0):
+        asel(R("ex", 512 * b, 512 * b + 512), "zer", [[-1, 32], [0, 16]], A.not_equal, 1.0, -32 * b, 1)
 
     def next_list(t):
         ts(NL, G("nxt", lst("jl", t)), 0.25 - LIFT, None, A.add)
@@ -290,202 +325,265 @@ def rank_program(g, core, T, topo):
     def tool_list(t):
         ts(AL, G("tool", lst("jl", t)), 0.25 - LIFT, None, A.add)
 
-    def numbers():
-        ts(NH, NL, LIFT, None, A.add)
-        cp(AH, AL)
-
-    def long_gather(out, win, first):
-        for c in range(0, 128, PIECE):
-            act(R(out, 16 * c, 16 * (c + PIECE)), G(win, R("anl", first + c, first + c + PIECE)))
+    def long_gather(out, win, first, a, b):
+        cuts = sorted({a, max(a, b)} | {c for c in OPT["cuts"].get(out, ()) if a < c < b})
+        for c, d in zip(cuts, cuts[1:]):
+            act(R(out, 16 * c, 16 * d), G(win, R("anl", first + c, first + d)))
 
     def limits(t):
         act("lg", G("lmt", lst("jl", t)))
-        if t:
-            mm(LT, "lg", "idb", True, True)
-            act("lgt", LT)
 
     def spread(t, b):
-        if t:
+        if b >= {"q": 4, "h": 2, "k": 0, "d": 0}[OPT["cmp"][t]]:
+            if b == 3:
+                mm(LIM, "idb", "lg", True, True)
+            return
+        if t and OPT["ex"]:
             mm("ps%d" % LB[b], "lgt", R("ex", 512 * b, 512 * b + 512), True, True)
-        for k in range(0 if t else 16):
+        for k in range(0 if t and OPT["ex"] else 16):
             mm(R("ps%d" % LB[b], k, 512, 16), "idb", R("lg", 32 * b, 32 * b + 32), True, True)
+
+    def wear(t, who):
+        for e, a, b in WEAR[t]:
+            if e == who:
+                cp(R("xa", 16 * a, 16 * b), G(XW, R("anl", a, b)), e)
 
     def compare(b):
         tt(R("ov", 512 * b, 512 * b + 512), R("xa", 512 * b, 512 * b + 512), "ps%d" % LB[b], A.is_gt)
 
-    def count(h):
-        lin(R(CNT, 64 * h, 64 * h + 64), [(R("ep", 16 - k, 144 - k), R("ov", 1024 * h + k, 1024 * h + 1024, 16)) for k in range(16)])
+    def turn_over(piece, src, rows, st):
+        for k in range(16):
+            mm(R(piece, k, 128, 16), R(src, k, 2048, 16), rows(k), st and k == 0, k == 15)
 
-    def pick(src, piece, h, first):
-        o = R(piece, 64 * h, 64 * h + 64)
-        lin(o, first + [(blk("fd", k), R(src, 1024 * h + k, 1024 * h + 1024, 16)) for k in range(16)])
+    def own(k):
+        return R("idb", k, 128, 16)
 
-    def first_pockets():
-        ts("mall", "pkt", 4095, None, A.bitwise_and)
-        for i in range(3):
-            ts((0, i), blk("pkt", i), 2.0, 2048.0 * (2 - i), A.mult, A.add)
-        tt("qa0", R(P01, 0, 384), "mall", A.subtract)
+    def least(out, piece):
+        scan(out, "rs", piece, A.max, A.min)
 
-    def update(t):
-        tt("qt", R(NP, 0, 256), blk("qa%d" % t, 0, 2), A.max)
-        ts(blk("qa%d" % (t + 1), 0, 2), "qt", NOTAG, None, A.bitwise_and)
+    def to_list(out, src):
+        ts(out, R(src, 15, 128, 16), 1 / 16, None, A.mult)
 
-    def arrived(t):
-        qa = "qa%d" % t
-        ts(blk("mall", 0, 2), blk(qa, 0, 2), MSK, None, A.bitwise_and)
-        ts(blk("mall", 2), blk(qa, 2), MSK, None, A.bitwise_and)
-        ts("q2c%d" % t, blk(qa, 2), NOIDX, None, A.bitwise_and)
+    def differences(b):
+        mm(R(DIF[b], 0, 256), "vh", blk("gs", 2 * b, 2), True, False)
+        for q in range(2):
+            mm(R(DIF[b], 128 * q, 128 * q + 128), blk("gsn", 2 * b + q), "vh", False, q == 1)
 
-    def evicted(t, q2):
-        tt("qv", P01, q2, A.max)
-        ts("mv", "qv", MSK, None, A.bitwise_and)
-        tt("al", P01, blk("qa%d" % t, 0), A.not_equal)
-        tt("be", P01, q2, A.is_gt)
+    def earlier(b):
+        tt(blk("eq", 2 * b, 2), R(DIF[b], 0, 256), "tri", A.is_equal)
+        for q in range(2 * b, 2 * b + 2):
+            mm(ZL, R("cb", 112 - 16 * q, 240 - 16 * q), blk("eq", q), False, q == 7)
 
+    def changes(at):
+        lin(at, [("id2k", "be"), ("idn4k", "al"), ("id4m", E[0]), ("idn4k", E[1]), ("idn4k", E[2])])
+        lin(R(at, 128, 256), [("idb", "be"), ("idb", "al"), ("id8k", E[1]), ("idn8m", E[0]), ("idn", E[2])])
+        act("ss", R(at, 0, 256), SIGN, bias=-1.5)
+
+    def new_pairs(t):
+        mm(R(NP, 0, 256), TWO, R("tags", rows=2), True, False)
+        for i in range(2):
+            lin((0, 1 + i), [("id8k", nexts(t)), ("idb", firsts(t)), ("cd", "idb"), ("cn", "id8k")], False, False)
+        for i in range(2):
+            mm((0, 1 + i), "id4m", blk("ss", i), False, i == 1)
+
+    cp("k15", "kgi")
+    for b in range(8):
+        ts(blk("gs", b), "ones", R("bo", 16 * b, 16 * b + 1), 1 / 16, A.mult, A.mult)
     cp(lst("jl", 0), "jmt")
+    chain.update(OPT["chain"])
+    cp("hi2", G("jtt", lst("jl", 0)))
+    ts("nxt", "jtt", 1 / 4096, LIFT - 0.22, A.mult, A.add)
+    ts("mv", "hi2", 4095, None, A.bitwise_and)
+    ts(NL, "hi2", 1 / 4096, 0.03, A.mult, A.add)
+    cp(AL, "mv")
     ts("tint", "jtt", 4095, None, A.bitwise_and)
     ts("tool", "tint", LIFT, None, A.add)
-    tool_list(0)
-    act("c4k", R("ones", 0, 2), SILU, scale=4096.0, more=1300)
+    long_gather("ng", "nxt", 128, 0, OPT["lgat"])
     limits(0)
-    follow(1)
-    cp(R("ep", 16, 144, 16), GROUPS)
-    cp("k15", "kgi")
-    ts("e16", GROUPS, 16.0, None, A.mult)
+    long_gather("ng", "nxt", 128, OPT["lgat"], EARLY[0])
     for b in range(4):
         spread(0, b)
-    for k in range(16):
-        act(R("fd", 129 * k, 128 * k + 128, 16), R("idb", k, 128, 16))
+    ts(nexts(0), NL, LIFT, None, A.add)
+    cp(firsts(0), AL)
 
     for t in range(NT):
-        last = t == NT - 1
+        first, last = t == 0, t == NT - 1
         jl, qa = lst("jl", t), "qa%d" % t
         q2 = R("q2c%d" % t) if t else blk(qa, 2)
-        for e, a, b in WEAR:
-            (cp if e == "v" else act)(R("xa", 16 * a, 16 * b), G(XW, R("anl", a, b)))
-        if t == 0:
-            ts("nint", "jtt", 12, None, A.logical_shift_right)
-            ts("nxt", "nint", LIFT, None, A.add)
-            next_list(0)
-            numbers()
-        compare(0)
-        compare(1)
-        count(0)
-        compare(2)
-        compare(3)
-        count(1)
+        AH, NH = firsts(t), nexts(t)
+        USED = [("idb", AH), ("cd", "idb")]
+        NEWS = [("idb", NH), ("cn", "idb")]
+        wear(t, "v")
+        wear(t, "s")
+        if first:
+            long_gather("sg", "sdt", 0, 0, 128)
+            long_gather("ng", "nxt", 128, EARLY[0], 96)
+        else:
+            long_gather("sg", "sdt", 0, SOON[t], 128)
+        mm(SIS, AH, "idb", True, False)
+        turn_over(SIS, "sg", own, False)
+        if OPT["sis"][t] == "s":
+            act("sis", SIS, IDN, -W / 2)
+        else:
+            mm(DU, "idw", "ones", True, False)
+            for k in range(16):
+                mm(R(DU, k, 128, 16), R("sg", k, 2048, 16), own(k), False, False)
+        act("wf", SIS, SIGN, bias=0.5 - W)
         mm(SUM, "idb", "tie", True, False)
-        for k in range(16):
-            mm(R(SUM, k, 128, 16), R("xa", k, 2048, 16), "e16", False, k == 15)
-        ts("cc", CNT, 9.0, None, A.is_ge)
-        long_gather("sg", "sdt", 0)
-        pick("sg", DU, 0, [])
-        pick("sg", DU, 1, [])
-        tt(DU, "cc", DU, A.mult)
-        tt("uw", AH, DU, A.add)
-        ts("wf", "uw", float(W), -float(W), A.is_ge, A.mult)
-        lin(UU, [("idb", "uw"), ("idb", "wf")])
-        scan("pre", "msk", SUM)
-        cp("key", SUM)
+        turn_over(SUM, "xa", lambda k: GROUPS, False)
+        if OPT["sis"][t] == "s":
+            lin(DU, [(AH, "idn"), ("idb", "sis"), ("idw", "wf")])
+        else:
+            mm(DU, "idw", "wf", False, True)
+        how = OPT["cmp"][t]
+        for b in range({"q": 4, "h": 2, "k": 0, "d": 0}[how]):
+            compare(b)
+        for a, b in {"q": (), "h": ((64, 128),), "k": ((0, 128),), "d": ((0, 64), (64, 128))}[how]:
+            for k in range(16):
+                tt(R("ov", 16 * a + k, 16 * b, 16), R("xa", 16 * a + k, 16 * b, 16), R(LIM, a, b), A.is_gt)
+        turn_over(CNT, "ov", lambda k: GROUPS, True)
+        if OPT["key"][t] == "s":
+            act("key", SUM)
+        long_gather("ng", "nxt", 128, EARLY[t] if t else max(96, EARLY[0]), 128)
+        scan("pre", "msk", SUM, A.mult, A.max)
+        if OPT["key"][t] == "v":
+            cp("key", SUM)
+        if t:
+            tt("qt", R(NP, 0, 256), blk("qa%d" % (t - 1), 0, 2), A.max)
+        else:
+            ts("mall", "pkt", 4095, None, A.bitwise_and)
         tt("gm", G("pre", "k15"), "key", A.is_equal)
-        if t == 0:
-            consts()
+        ts("cc", CNT, 16 * 9.0, None, A.is_ge)
         mm(OH, "gm", "idb", True, True)
-        mm(LT, "gm", "idb", True, True)
-        act("ohs", LT)
+        ahead = EARLY[t] >= 96 and not last
+        NW, JL = ((5, 1), (5, 2)) if ahead else ((3, 1), (5, 2)) if OPT["nw"] else ((5, 1), (3, 1))
+
+        def jobs():
+            mm(DN, NH, "idn", True, False)
+            turn_over(DN, "ng", own, False)
+            tt("cn", "cc", DN, A.mult)
+            if not last:
+                lin(NW, [("gm", "id8k")] + NEWS)
+                if OPT["sc"] != 3 or ahead:
+                    table()
+                above(OPT["nh"][t], "nh", NW, 8192.0 + LIFT)
+                lin(JL, [("idb", "dm"), ("bo", "nh")])
+                least("js", JL)
+                to_list(lst("jl", t + 1), "js")
+
+        def table():
+            lin(NN, NEWS)
+            act("nf", NN)
+            put(G("nxt", jl), "nf")
+
+        if ahead:
+            jobs()
         if t:
-            update(t - 1)
+            ts(blk(qa, 0, 2), "qt", NOTAG, None, A.bitwise_and)
+            tt("cd", "cc", DU, A.mult)
+            ts(blk("mall", 0, 2), "qt", MSK, None, A.bitwise_and)
+            ts(blk("mall", 2), blk(qa, 2), MSK, None, A.bitwise_and)
         else:
-            first_pockets()
-        tt(P01, blk(qa, 0), blk(qa, 1), A.max)
-        if t:
-            arrived(t)
-        evicted(t, q2)
-        tt("omv", "mv", OH, A.mult)
-        lin(UN, [("idb", "uw"), ("idb", "wf")])
-        if last:
-            act(blk("un", 0), UN, scale=2.0)
-        else:
+            for i in range(3):
+                ts((0, i), blk("pkt", i), 2.0, 2048.0 * (2 - i), A.mult, A.add)
+            ts("rtn", "rtb", -1.0, None, A.mult)
+            tt("qa0", R(P01, 0, 384), "mall", A.subtract)
+            tt("cd", "cc", DU, A.mult)
+            tt(P01, blk(qa, 0), blk(qa, 1), A.max)
+        lin(UU, USED)
+        if OPT["un"] and not last:
+            lin(UN, USED)
             act("uf", UN, IDN, bias=LIFT)
-        lin(MISS, [("id4m", "ones")], sp=False)
+            put(G("tool", jl), "uf")
+        lin(UH, [("gm", "id8k")] + USED)
         for i in range(3):
             tt(E[i], blk("mall", i), UU, A.is_equal)
-            mm(MISS, "idn8m", E[i], False, i == 2)
-        lin(AUP, [("idb", "omv")] + [("id4m", x) for x in E])
-        tt("ohu", "ohs", UU, A.mult)
-        long_gather("ng", "nxt", 128)
-        for h in range(2):
-            pick("ng", DN, h, [("idn", R("an", 128 + 64 * h, 192 + 64 * h))])
-        if last:
-            tt("g12", "qv", MISS, A.min)
-            give(t, "g12", q2, "land")
-        tt("x1", "ohu", MISS, A.max)
-        tt("vh", "x1", AUP, A.min)
-        tt(DN, "cc", DN, A.mult)
-        tt(blk("un", 1) if last else "nf", NH, DN, A.add)
-        if not last:
-            tt("nh", "nf", OH, A.mult)
-            lin(R(JL, 0, 8), [(R("ep", 16 - r, 144 - r), R("nh", r, 128, 16)) for r in range(16)])
-            tt("g1%d" % t, "qv", MISS, A.min)
-            give(t, "g1%d" % t, q2, blk("qa%d" % (t + 1), 2))
-            ts(lst("jl", t + 1), R(JL, 0, 8), -LIFT, None, A.add)
+        if OPT["un"] == 0 and not last:
+            act("uf", UU, IDN, bias=LIFT)
             put(G("tool", jl), "uf")
-            put(G("nxt", jl), "nf")
-            act(blk("un", 1), "nf")
+        lin(MARK, [("gm", "id2k")] + [("idn8m", x) for x in E])
+        lin(AUP, [("id8k", x) for x in E], sp=False)
+        if t:
+            ts("q2c%d" % t, blk(qa, 2), NOIDX, None, A.bitwise_and)
+            tt(P01, blk(qa, 0), blk(qa, 1), A.max)
+        above(OPT["ohu"][t], "ohu", UH, 8192.0)
+        tt("qv", P01, q2, A.max)
+        ts("mv", "qv", MSK, None, A.bitwise_and)
+        tt("g1%d" % t, "qv", MARK, A.add)
+        give(t, "g1%d" % t, q2, "land" if last else blk("qa%d" % (t + 1), 2))
+        tt("omv", "mv", OH, A.mult)
+        mm(AUP, "idb", "omv", False, True)
+        tt("x1", "ohu", MARK, A.max)
+        tt("al", P01, blk(qa, 0), A.not_equal)
+        tt("be", P01, q2, A.is_gt)
+        if OPT["sc"] == 1:
+            changes(SC)
+        if not ahead:
+            jobs()
+        if OPT["sc"] == 3:
+            changes(SUM)
+            if not last and not ahead:
+                table()
+        tt("vh", "x1", AUP, A.min)
+        for b in range(3):
+            differences(b)
+        lin(VL, [("idb", "dm"), ("bo", "vh")])
+        lin(ZL, [("idb", "dm"), ("bo", "vh")], sp=False)
+        least("vs", VL)
+        if not last:
+            if OPT["nfirst"][t] == "n":
+                next_list(t + 1)
+                long_gather("ng", "nxt", 128, 0, EARLY[t + 1])
             tool_list(t + 1)
-        lin(OM, [("idb", "ohs")] + [("idn", x) for x in E])
-        act("ohm", OM, RELU)
-        for r in range(16):
-            mm(top(R(VL, r, 128, 16)), R("vh", 8 * r, 8 * r + 8), GROUPS, True, True)
-        cp(top("v8"), top(VL))
-        for b in range(2):
-            bank = "ps%d" % (6 + b)
-            mm(bank, "vh", R("gs", 512 * b, 512 * b + 512), True, False)
-            for q in range(4):
-                mm(blk(bank, q), blk("gsn", 4 * b + q), "vh", False, q == 3)
-        mm(R(VL, 0, 8), top("v8"), top(R("idb", 0, 8)), True, True)
-        mm(R(ZL, 0, 8), top("v8"), top(R("idb", 0, 8)), True, False)
-        for q in range(8):
-            mm(R(SR, 16 * q, 16 * q + 16), "bo", R("ohm", q, 128, 8), True, True)
-        ts("shf", SR, R("rtn", t, t + 1), R("rtf", t, t + 1), A.mult, A.add)
-        tt(R("eq", 0, 512), "ps6", "tri", A.is_equal)
-        tt(R("eq", 512, 1024), "ps7", "tri", A.is_equal)
-        cp(lst("vl", t), R(VL, 0, 8))
-        for q in range(8):
-            mm(R(ZL, q, q + 1), R("eq", q, 1024, 8), R("c4k", 0, 1), False, q == 7)
-        tt("yy", G(XW, lst("vl", t)), "shf", A.add)
-        tt("off", R(ZL, 0, 8), "spare", A.min)
+            limits(t + 1)
+            long_gather("sg", "sdt", 0, 0, SOON[t + 1])
+            if OPT["ex"]:
+                mm(LT, "lg", "idb", True, True)
+                act("lgt", LT)
+        lin(SR, [("id2k", "cn15"), ("bo", "x1")])
+        earlier(0)
+        differences(3)
+        earlier(1)
+        to_list(lst("vl", t), "vs")
+        if OPT["sc"] == 0:
+            changes(SUM)
+        earlier(2)
+        earlier(3)
+        new_pairs(t)
+        ts("shf", SR, R("rtn", t, t + 1), 8.0, A.max, A.min)
+        if not last and OPT["nfirst"][t] != "n":
+            next_list(t + 1)
+            long_gather("ng", "nxt", 128, 0, EARLY[t + 1])
+        tt("yy", G(XW, lst("vl", t)), "shf", A.subtract)
+        def finish():
+            tt("y1", R(NP, 0, 256), blk(qa, 0, 2), A.max)
+            act("un", "y1", IDN, LIFT - 0.36, 1 / 8192)
+            mm(R(NQ, 0, 256), TWO, R("ends", rows=2), True, False)
+            mm(R(NQ, 0, 256), "idn1m", "ss", False, False)
+            mm(R(NQ, 0, 256), "idn4k", "un", False, True)
+
+        if last and OPT["fin"]:
+            finish()
+        least("os_", ZL)
         ts("yc", "yy", 0.0, 255.0, A.max, A.min)
-        cp(lst("ofl", t), "off")
+        to_list(lst("ofl", t), "os_")
+        if not last:
+            cp(firsts(t + 1), AL)
+            ts(nexts(t + 1), NL, LIFT, None, A.add)
         cp(G("xt", lst("ofl", t)), "yc")
         if last:
             store("y", T.yx[:, :], XW, "ox")
-        lin(SC0, [("idb", "be"), ("idn", "al"), ("id8k", E[0]), ("idn", E[1]), ("idn", E[2])])
-        lin(SC1, [("idb", "be"), ("idb", "al"), ("idn", "ones"), ("id8k", E[1]), ("idn8m", E[0]), ("idn", E[2])])
-        act("ss", R(SC0, 0, 256), SIGN, bias=-0.5)
-        tool = [("idb", blk("un", 0))] if last else [("idb", "uw"), ("idb", "wf")]
-        new = [[("id8k", ("c50", "c25")[i]), ("id8k", blk("un", 1)), ("idn8m", "ones")] + tool for i in range(2)]
-        if not last:
-            limits(t + 1)
-            for b in range(4):
-                spread(t + 1, b)
-            next_list(t + 1)
-            numbers()
-        for i in range(2):
-            lin((0, 1 + i), new[i] + [("id4m", blk("ss", i))])
-        if last:
-            for i in range(2):
-                lin((5, 1 + i), new[i] + [("id4m", "ones"), ("idn4m", blk("ss", i))])
-            tt("qm", blk(qa, 0, 2), blk("mall", 0, 2), A.add)
-            tt("y1", R(NP, 0, 256), "qm", A.max)
-            tt("y2", R(NQ, 0, 256), "y1", A.min)
-            for i in range(2):
-                act(blk("yo", i), blk("y2", i), IDN, bias=-1024.0 * (2 - i), scale=0.5)
-            store("s", T.yp[:, 0:256], R("yo"), "op")
+            if not OPT["fin"]:
+                finish()
             ts("hi2", "land", 1, -4096, A.logical_shift_right, A.bitwise_and)
             ts("mv", "land", MSK, None, A.bitwise_and)
+            tt("yo", R(NQ, 0, 256), "y1", A.add)
+            store("s", T.yp[:, 0:256], R("yo"), "op")
             tt("y3", "hi2", "mv", A.add)
-            store("s", T.yp[:, 256:384], R("y3"), "oq")
+            store("y", T.yp[:, 256:384], R("y3"), "oq")
+        else:
+            for b in range(4):
+                spread(t + 1, b)
     issue()
     for sem in ("sv", "ss", "sp", "sg"):
         g.wait_ge(T.sem[sem], cnt[sem])

from concourse.bass import DstId, RemoteDMATransfer
from concourse.mybir import AluOpType, ActivationFunctionType

A = AluOpType
CPY = ActivationFunctionType.Copy
IDN = ActivationFunctionType.Identity
RELU = ActivationFunctionType.Relu
SIGN = ActivationFunctionType.Sign
SILU = ActivationFunctionType.Silu
W, MA, J, NT = 1792, 128, 384, 3
WEAR = [(("v", 0, 64), ("v", 64, 128)),
        (("v", 0, 64), ("s", 64, 128)),
        (("v", 0, 32), ("s", 48, 96), ("v", 32, 48), ("s", 96, 128))]
EARLY = [128, 0, 0]
SOON = [0, 128, 128]
LIFT = 1024.0
BIG = 4194304.0
LB = (5, 4, 6, 7)
CYCLE, GATHER, SCATTER, LATE, DMA, RATE, FAR, FIRST = 0.85, 1.35, 2.6, 140, 1500, 400, 3500, 5500
CALL = {"v": (10, 50), "s": (75, 100), "g": (150, 0)}
PIPE = 150
ROUNDS = 6
ORDER = []
OPT = dict(key="vvv", ohu="vvv", nh="vv", ids=5, sc=0, cmp="qqq", fin=1, un=1, ex=0, sis="sps", cuts={}, nw=1, nfirst="aa", lgat=64, chain="", loads="yjt yxw ylm ysd ypk yrt")

_B, _H, _F, _I, _U = "bfloat16", "float16", "float32", "int32", "uint16"
SCRATCH = {}
for _names, _w, _d in (
        ("sdt", W, _B), ("xt", W + 8 * MA, _B), ("lmt", J, _B), ("rtb", NT, _B), ("rtn", NT, _F), ("nxt tool", J, _F),
        ("jtt pkt tint mall qa0 qa1 qa2", J, _I), ("jmt kgi", 8, _I), ("jl vl ofl", 8 * NT, _U), ("anl", 256, _U),
        ("xa sg ov ex", 2048, _B), ("ng", 2048, _H), ("pre key msk y3 uf nf rs js vs os_", 128, _F),
        ("gm lg lgt cc al be wf shf yy yc", 128, _B), ("ee", 384, _B), ("ss tags ends", 256, _B), ("an", 512, _H), ("un", 256, _H),
        ("sis cd cn nh omv ohu x1 vh", 128, _H), ("qv mv q2c1 q2c2 g10 g11 g12 land hi2", 128, _I), ("y1 yo", 256, _F),
        ("qt", 256, _I), ("zer", 512, _B), ("tri", 256, _B), ("k15", 8, _U), ("cb", 240, _B),
        ("ones cn15 idb idn idw id2k id8k id4m idn4k idn1m idn8m bt bo tie sel dm", 128, _B), ("gs gsn eq", 1024, _B)):
    for _n in _names.split():
        SCRATCH[_n] = ("sbuf", [128, _w], _d)
for _k in range(8):
    SCRATCH["ps%d" % _k] = ("psum", [128, 512], _F)
SEMAPHORES = ["sv", "ss", "sp", "sg", "ljm", "ljt", "llm", "lpk", "lrt", "lxw", "lsd", "a0", "a1", "a2", "sent", "ox", "op", "oq"]
MSK, NOIDX, NOTAG = 2047, 4188159, 4194303
P01, NP = (0, 0), (0, 1)
CNT, VL, UH, OH, ZL = (1, 0), (1, 0), (1, 1), (1, 2), (1, 3)
SUM, UN, NN = (2, 0), (2, 2), (2, 3)
DU, SIS, LT, SR = (3, 0), (3, 1), (3, 3), (3, 2)
UU, SC = (4, 0), (4, 0)
DN, NQ = (5, 0), (5, 1)
MARK = (6, 0)
AUP, LIM = (7, 0), (7, 1)
DIF = ((7, 0), (6, 0), (4, 0), (7, 2))


def rank_program(g, core, T, topo):
    rank = T.rank_of(core)
    if rank is None:
        return
    nxt_core = T.cores[(rank + 1) % len(T.cores)]
    prv_core = T.cores[(rank - 1) % len(T.cores)]
    rid, pid = topo.addr(nxt_core, core)
    mask = topo.mask(core, nxt_core)
    nrec = len(topo.engines(prv_core, core))

    ENG = {"v": g.vector, "s": g.scalar, "p": g.tensor, "g": g, "y": g.sync}
    OWN = {"v": "sv", "s": "ss", "p": "sp", "g": "sg"}
    cnt = {"sv": 0, "ss": 0, "sp": 0, "sg": 0}
    clk = {e: {} for e in ENG}
    snap = {}
    calls = []
    moved = [0]
    chain, before = set(), {}
    used, turn = {}, {}

    def R(x, a=0, b=None, step=1, rows=128):
        if isinstance(x, str):
            b = SCRATCH[x][1][1] if b is None else b
            return T[x][0:rows, a:b:step], [(x, frozenset(range(a, b, step)))]
        if isinstance(x[0], int):
            base = 128 * x[1]
            return R("ps%d" % x[0], base + a, base + (128 if b is None else b), step)
        return x

    def G(win, off):
        win, off = R(win), R(off)
        return win[0].indirect(off[0]), win[1], off[1]

    def wait(e, toks):
        for tk in sorted(toks, key=lambda q: (-len(snap[q]), q)):
            sem, val = tk
            if clk[e].get(sem, 0) >= val:
                continue
            if any(o != tk and snap[o].get(sem, 0) >= val and clk[e].get(o[0], 0) < o[1] for o in toks):
                continue
            ENG[e].wait_ge(T.sem[sem], val)
            for a, b in snap[tk].items():
                if clk[e].get(a, 0) < b:
                    clk[e][a] = b

    def span(e, outs, ins, per):
        n = len(outs[0][1][0][1])
        if e == "p":
            return 3 + max(64, n) * CYCLE / 2
        if len(outs[0]) > 2:
            return CALL[e][1] + 16 * len(outs[0][2][0][1]) * SCATTER
        if ins and len(ins[0]) > 2:
            return CALL[e][1] + n * GATHER
        if per is None:
            per = 0.5 if e == "v" and all(SCRATCH[x[1][0][0]][2] in (_B, _H, _U) for x in outs + ins[:1]) else 1
        return CALL[e][0] + max(64, n * per) * CYCLE

    def op(e, call, outs, ins, token=None, late=None, after=(), per=None, more=0):
        acc = []
        for o in outs:
            acc += [(nm, c, True) for nm, c in o[1]] + [(nm, c, False) for x in o[2:] for nm, c in x]
        for o in ins:
            acc += [(nm, c, False) for x in o[1:] for nm, c in x]
        me, hard, soft = len(calls), set(after), set()
        for nm, c, wrt in acc:
            old = used.get(nm, [])
            if SCRATCH[nm][0] == "psum":
                if old and old[-1][0] != me and calls[old[-1][0]]["e"] != e:
                    turn[nm], old = [u[0] for u in old], []
                hard.update(turn.get(nm, ()))
                if e == "p":
                    soft.update(u[0] for u in old[-1:])
            for i, c2, wrt2 in old:
                if i != me and (wrt or wrt2) and c & c2:
                    same = calls[i]["e"] == e and token is None and calls[i]["token"] is None
                    (soft if same and (e == "p" or not wrt2) else hard).add(i)
            used[nm] = [u for u in old if not (wrt and u[1] <= c)] + [(me, c, wrt)]
        if e in chain:
            soft.update(i for i in range(me) if calls[i]["e"] == e and i >= before.get(e, 0))
            before[e] = me
        busy = more + (span(e, outs, ins, per) if token is None else 60 if call else 0)
        calls.append(dict(e=e, call=call, busy=busy, late=LATE + (PIPE if e == "p" else 0) if late is None else late, token=token, hard=hard, soft=soft - hard - {me}))
        return me

    def place(order, back):
        need = [[] for _ in calls]
        for i, c in enumerate(calls):
            for j in c["hard"] | c["soft"]:
                a, b = (i, j) if back else (j, i)
                need[b].append((a, calls[j]["late"] if j in c["hard"] else 0))
        taken, end = {e: [] for e in "vspgyr"}, [None] * len(calls)

        def fit(i):
            for j, lag in need[i]:
                if end[j] is None:
                    fit(j)
            at, busy = max([end[j] + lag for j, lag in need[i]] + [calls[i]["late"] if back else 0]), calls[i]["busy"]
            line = taken[calls[i]["e"]]
            k = 0
            while k < len(line) and line[k][0] < at + busy:
                at, k = max(at, line[k][1]), k + 1
            line.insert(k, (at, at + busy))
            end[i] = at + busy

        for i in order:
            if end[i] is None:
                fit(i)
        return end

    def issue():
        every = range(len(calls))
        if not ORDER:
            end, best = place(every, False), None
            for rnd in range(ROUNDS):
                end = place(sorted(every, key=lambda i: (-end[i], -i)), True)
                end = place(sorted(every, key=lambda i: (-end[i], i)), False)
                total = max(end[i] + calls[i]["late"] for i in every)
                if best is None or total < best:
                    best, ORDER[:] = total, sorted(every, key=lambda i: (end[i] - calls[i]["busy"], end[i], i))
        for i in ORDER:
            c = calls[i]
            e = c["e"]
            known = {}
            if e != "r":
                wait(e, {calls[j]["token"] for j in c["hard"]})
                done = c["call"]()
                if c["token"] is None:
                    cnt[OWN[e]] += 1
                    c["token"] = (OWN[e], cnt[OWN[e]])
                    done.then_inc(T.sem[OWN[e]], 1)
                known = dict(clk[e])
            if c["token"]:
                known[c["token"][0]] = c["token"][1]
                snap[c["token"]] = known

    def size(x):
        return 128 * len(x[1][0][1]) * (4 if SCRATCH[x[1][0][0]][2] in (_I, _F) else 2)

    def load(e, nm, src, sem, b=None):
        o = R(nm, 0, b)
        moved[0] += size(o)
        i = op(e, lambda: ENG[e].dma_start(o[0], src[:, :]).then_inc(T.sem[sem], 16), [o], [], (sem, 16), DMA + moved[0] / RATE)
        calls[i]["soft"].update(range(i))

    def store(e, dst, x, sem):
        op(e, lambda: ENG[e].dma_start(dst, x[0]).then_inc(T.sem[sem], 16), [], [x], (sem, 16), DMA + size(x) / RATE)

    def give(t, a, b, dst):
        a, b, dst = R(a), R(b), R(dst)
        move = RemoteDMATransfer(dst_ids=[DstId(rid=rid, pnc=pid)], dma_engine_mask=mask, remote_sem=T.sem["a%d" % t],
                                 srcs=[a[0], b[0]], dsts=[dst[0]], alu_op=2)
        i = op("g", lambda: g.remote_dma_fused([move], local_sem=T.sem.sent), [], [a, b], False, FAR, more=0 if t else FIRST)
        op("r", None, [dst], [], ("a%d" % t, nrec), LATE, [i])

    def col(x):
        return x[0] if isinstance(x, tuple) else x

    def cols(*xs):
        return [x for x in xs if isinstance(x, tuple)]

    def tt(out, a, b, o):
        out, a, b = R(out), R(a), R(b)
        both = SCRATCH[a[1][0][0]][0] == SCRATCH[b[1][0][0]][0]
        op("v", lambda: g.vector.tensor_tensor(out[0], a[0], b[0], o), [out], [a, b], per=1 + both)

    def ts(out, a, s1, s2, *o):
        out, a = R(out), R(a)
        op("v", lambda: g.vector.tensor_scalar(out[0], a[0], col(s1), col(s2), *o), [out], [a] + cols(s1, s2))

    def cp(out, a, e="v"):
        if e == "s":
            return act(out, a)
        out, a = R(out), R(a)
        op("v", lambda: g.vector.tensor_copy(out[0], a[0]), [out], [a])

    def scan(out, a, b, o0, o1):
        out, a, b = R(out), R(a), R(b)
        op("v", lambda: g.vector.tensor_tensor_scan(out[0], a[0], b[0], 0.0, o0, o1), [out], [a, b])

    def act(out, a, func=CPY, bias=0.0, scale=1.0):
        out, a = R(out), R(a)
        op("s", lambda: g.scalar.activation(out[0], a[0], func, bias=bias, scale=scale), [out], [a], more=1300 if func is SILU else 0)

    def put(out, a):
        a = R(a)
        op("s", lambda: g.scalar.activation(out[0], a[0], SILU), [out], [a])

    def above(e, out, a, c):
        if e == "v":
            ts(out, a, -c, 0.0, A.add, A.max)
        else:
            act(out, a, RELU, bias=-c)

    def mm(out, l, r, st, sp):
        out, l, r = R(out), R(l), R(r)
        op("p", lambda: g.tensor.matmul(out[0], l[0], r[0], st, sp), [out], [l, r])

    def lin(out, terms, st=True, sp=True):
        for i, (l, r) in enumerate(terms):
            mm(out, l, r, st and i == 0, sp and i == len(terms) - 1)

    def fill(x, c):
        x = R(x)
        op("v", lambda: g.vector.memset(x[0], c), [x], [])

    def asel(out, in_, pat, cmp_, f, base, cm):
        out, in_ = R(out), R(in_)
        op("g", lambda: g.affine_select(out[0], in_[0], pat, cmp_, f, base, cm), [out], [in_], per=2)

    def iota(out, pat, base, cm):
        o = R(out)
        op("g", lambda: g.iota(o[0], pat, base, cm, allow_small_or_imprecise_dtypes=SCRATCH[o[1][0][0]][2] != _I), [o], [], per=2)

    def blk(x, i, n=1):
        return R(x, 128 * i, 128 * (i + n))

    def lst(nm, t):
        return R(nm, 8 * t, 8 * t + 8)

    XW = R("xt", 0, W)
    AL, NL = blk("anl", 0), blk("anl", 1)
    E = [blk("ee", i) for i in range(3)]
    GROUPS = R("bo", 0, 128, 16)
    TWO = R("ones", rows=2)

    def firsts(t):
        return blk("an", 2 * (t % 2))

    def nexts(t):
        return blk("an", 2 * (t % 2) + 1)

    load("s", "jmt", T.jm, "ljm")
    for nm in OPT["loads"].split():
        load(nm[0], {"rt": "rtb", "xw": "xt"}.get(nm[1:], nm[1:] + "t"), T[nm[1:]], "l" + nm[1:], W if nm[1:] == "xw" else None)

    fill("zer", 0.0)
    fill("ones", 1.0)
    fill("cb", 0.0)
    iota("kgi", [[16, 8]], 15, 0)
    asel("bt", blk("zer", 0), [[16, 8], [0, 16]], A.is_gt, 16.0, 0, -1)
    asel("bo", "bt", [[16, 8], [0, 16]], A.is_ge, 0.0, 15, -1)
    asel("idb", "ones", [[-1, 128]], A.is_equal, 0.0, 0, 1)
    iota("tie", [[0, 8], [-1, 16]], 15, 0)
    asel("msk", "ones", [[0, 8], [1, 16]], A.is_gt, 0.0, 0, 0)
    asel("sel", "ones", [[0, 8], [1, 16]], A.is_equal, 0.0, 0, -1)
    act(R("cb", 112, 128), R("ones", 0, 16), SILU, scale=65536.0)
    for i, (nm, c) in enumerate((("idn", -1.0), ("idw", -W / 2), ("id2k", 2048.0), ("id8k", 8192.0), ("idn8m", -2 * BIG), ("id4m", BIG),
                                 ("idn4k", -4096.0), ("idn1m", -BIG / 4))):
        if i < OPT["ids"]:
            act(nm, "idb", scale=c)
        else:
            asel(nm, blk("zer", 0), [[-1, 128]], A.not_equal, c, 0, 1)
    mm(P01, "sel", "sel", True, True)
    act("dm", P01, IDN, BIG, -BIG)
    iota("cn15", [[0, 128]], -15, 0)
    iota("rs", [[16, 8], [0, 16]], 16 * W, 128)
    asel("rs", "rs", [[0, 8], [1, 16]], A.is_equal, 0.0, 0, 0)
    for b in range(2):
        half = R("gsn", 512 * b, 512 * b + 512)
        asel(half, "zer", [[16, 4], [0, 128]], A.is_gt, -1.0, 64 * b, -1)
        asel(half, half, [[16, 4], [0, 128]], A.is_ge, 0.0, 64 * b + 15, -1)
    asel("tri", blk("zer", 0, 2), [[0, 2], [1, 128]], A.is_gt, 0.5, 0, -1)
    for i in range(2):
        tag = 2048 * (2 - i)
        iota(R("tags", 128 * i, 128 * i + 128, rows=2), [[0, 128]], -2 * int(BIG), 2 * int(BIG) + tag)
        iota(R("ends", 128 * i, 128 * i + 128, rows=2), [[0, 128]], 3 * int(BIG) // 4, -3 * int(BIG) // 4 - tag)
    for b in range(4 if OPT["ex"] else 0):
        asel(R("ex", 512 * b, 512 * b + 512), "zer", [[-1, 32], [0, 16]], A.not_equal, 1.0, -32 * b, 1)

    def next_list(t):
        ts(NL, G("nxt", lst("jl", t)), 0.25 - LIFT, None, A.add)

    def tool_list(t):
        ts(AL, G("tool", lst("jl", t)), 0.25 - LIFT, None, A.add)

    def long_gather(out, win, first, a, b):
        cuts = sorted({a, max(a, b)} | {c for c in OPT["cuts"].get(out, ()) if a < c < b})
        for c, d in zip(cuts, cuts[1:]):
            act(R(out, 16 * c, 16 * d), G(win, R("anl", first + c, first + d)))

    def limits(t):
        act("lg", G("lmt", lst("jl", t)))

    def spread(t, b):
        if b >= {"q": 4, "h": 2, "k": 0, "d": 0}[OPT["cmp"][t]]:
            if b == 3:
                mm(LIM, "idb", "lg", True, True)
            return
        if t and OPT["ex"]:
            mm("ps%d" % LB[b], "lgt", R("ex", 512 * b, 512 * b + 512), True, True)
        for k in range(0 if t and OPT["ex"] else 16):
            mm(R("ps%d" % LB[b], k, 512, 16), "idb", R("lg", 32 * b, 32 * b + 32), True, True)

    def wear(t, who):
        for e, a, b in WEAR[t]:
            if e == who:
                cp(R("xa", 16 * a, 16 * b), G(XW, R("anl", a, b)), e)

    def compare(b):
        tt(R("ov", 512 * b, 512 * b + 512), R("xa", 512 * b, 512 * b + 512), "ps%d" % LB[b], A.is_gt)

    def turn_over(piece, src, rows, st):
        for k in range(16):
            mm(R(piece, k, 128, 16), R(src, k, 2048, 16), rows(k), st and k == 0, k == 15)

    def own(k):
        return R("idb", k, 128, 16)

    def least(out, piece):
        scan(out, "rs", piece, A.max, A.min)

    def to_list(out, src):
        ts(out, R(src, 15, 128, 16), 1 / 16, None, A.mult)

    def differences(b):
        mm(R(DIF[b], 0, 256), "vh", blk("gs", 2 * b, 2), True, False)
        for q in range(2):
            mm(R(DIF[b], 128 * q, 128 * q + 128), blk("gsn", 2 * b + q), "vh", False, q == 1)

    def earlier(b):
        tt(blk("eq", 2 * b, 2), R(DIF[b], 0, 256), "tri", A.is_equal)
        for q in range(2 * b, 2 * b + 2):
            mm(ZL, R("cb", 112 - 16 * q, 240 - 16 * q), blk("eq", q), False, q == 7)

    def changes(at):
        lin(at, [("id2k", "be"), ("idn4k", "al"), ("id4m", E[0]), ("idn4k", E[1]), ("idn4k", E[2])])
        lin(R(at, 128, 256), [("idb", "be"), ("idb", "al"), ("id8k", E[1]), ("idn8m", E[0]), ("idn", E[2])])
        act("ss", R(at, 0, 256), SIGN, bias=-1.5)

    def new_pairs(t):
        mm(R(NP, 0, 256), TWO, R("tags", rows=2), True, False)
        for i in range(2):
            lin((0, 1 + i), [("id8k", nexts(t)), ("idb", firsts(t)), ("cd", "idb"), ("cn", "id8k")], False, False)
        for i in range(2):
            mm((0, 1 + i), "id4m", blk("ss", i), False, i == 1)

    cp("k15", "kgi")
    for b in range(8):
        ts(blk("gs", b), "ones", R("bo", 16 * b, 16 * b + 1), 1 / 16, A.mult, A.mult)
    cp(lst("jl", 0), "jmt")
    chain.update(OPT["chain"])
    cp("hi2", G("jtt", lst("jl", 0)))
    ts("nxt", "jtt", 1 / 4096, LIFT - 0.22, A.mult, A.add)
    ts("mv", "hi2", 4095, None, A.bitwise_and)
    ts(NL, "hi2", 1 / 4096, 0.03, A.mult, A.add)
    cp(AL, "mv")
    ts("tint", "jtt", 4095, None, A.bitwise_and)
    ts("tool", "tint", LIFT, None, A.add)
    long_gather("ng", "nxt", 128, 0, OPT["lgat"])
    limits(0)
    long_gather("ng", "nxt", 128, OPT["lgat"], EARLY[0])
    for b in range(4):
        spread(0, b)
    ts(nexts(0), NL, LIFT, None, A.add)
    cp(firsts(0), AL)

    for t in range(NT):
        first, last = t == 0, t == NT - 1
        jl, qa = lst("jl", t), "qa%d" % t
        q2 = R("q2c%d" % t) if t else blk(qa, 2)
        AH, NH = firsts(t), nexts(t)
        USED = [("idb", AH), ("cd", "idb")]
        NEWS = [("idb", NH), ("cn", "idb")]
        wear(t, "v")
        wear(t, "s")
        if first:
            long_gather("sg", "sdt", 0, 0, 128)
            long_gather("ng", "nxt", 128, EARLY[0], 96)
        else:
            long_gather("sg", "sdt", 0, SOON[t], 128)
        mm(SIS, AH, "idb", True, False)
        turn_over(SIS, "sg", own, False)
        if OPT["sis"][t] == "s":
            act("sis", SIS, IDN, -W / 2)
        else:
            mm(DU, "idw", "ones", True, False)
            for k in range(16):
                mm(R(DU, k, 128, 16), R("sg", k, 2048, 16), own(k), False, False)
        act("wf", SIS, SIGN, bias=0.5 - W)
        mm(SUM, "idb", "tie", True, False)
        turn_over(SUM, "xa", lambda k: GROUPS, False)
        if OPT["sis"][t] == "s":
            lin(DU, [(AH, "idn"), ("idb", "sis"), ("idw", "wf")])
        else:
            mm(DU, "idw", "wf", False, True)
        how = OPT["cmp"][t]
        for b in range({"q": 4, "h": 2, "k": 0, "d": 0}[how]):
            compare(b)
        for a, b in {"q": (), "h": ((64, 128),), "k": ((0, 128),), "d": ((0, 64), (64, 128))}[how]:
            for k in range(16):
                tt(R("ov", 16 * a + k, 16 * b, 16), R("xa", 16 * a + k, 16 * b, 16), R(LIM, a, b), A.is_gt)
        turn_over(CNT, "ov", lambda k: GROUPS, True)
        if OPT["key"][t] == "s":
            act("key", SUM)
        long_gather("ng", "nxt", 128, EARLY[t] if t else max(96, EARLY[0]), 128)
        scan("pre", "msk", SUM, A.mult, A.max)
        if OPT["key"][t] == "v":
            cp("key", SUM)
        if t:
            tt("qt", R(NP, 0, 256), blk("qa%d" % (t - 1), 0, 2), A.max)
        else:
            ts("mall", "pkt", 4095, None, A.bitwise_and)
        tt("gm", G("pre", "k15"), "key", A.is_equal)
        ts("cc", CNT, 16 * 9.0, None, A.is_ge)
        mm(OH, "gm", "idb", True, True)
        ahead = EARLY[t] >= 96 and not last
        NW, JL = ((5, 1), (5, 2)) if ahead else ((3, 1), (5, 2)) if OPT["nw"] else ((5, 1), (3, 1))

        def jobs():
            mm(DN, NH, "idn", True, False)
            turn_over(DN, "ng", own, False)
            tt("cn", "cc", DN, A.mult)
            if not last:
                lin(NW, [("gm", "id8k")] + NEWS)
                if OPT["sc"] != 3 or ahead:
                    table()
                above(OPT["nh"][t], "nh", NW, 8192.0 + LIFT)
                lin(JL, [("idb", "dm"), ("bo", "nh")])
                least("js", JL)
                to_list(lst("jl", t + 1), "js")

        def table():
            lin(NN, NEWS)
            act("nf", NN)
            put(G("nxt", jl), "nf")

        if ahead:
            jobs()
        if t:
            ts(blk(qa, 0, 2), "qt", NOTAG, None, A.bitwise_and)
            tt("cd", "cc", DU, A.mult)
            ts(blk("mall", 0, 2), "qt", MSK, None, A.bitwise_and)
            ts(blk("mall", 2), blk(qa, 2), MSK, None, A.bitwise_and)
        else:
            for i in range(3):
                ts((0, i), blk("pkt", i), 2.0, 2048.0 * (2 - i), A.mult, A.add)
            ts("rtn", "rtb", -1.0, None, A.mult)
            tt("qa0", R(P01, 0, 384), "mall", A.subtract)
            tt("cd", "cc", DU, A.mult)
            tt(P01, blk(qa, 0), blk(qa, 1), A.max)
        lin(UU, USED)
        if OPT["un"] and not last:
            lin(UN, USED)
            act("uf", UN, IDN, bias=LIFT)
            put(G("tool", jl), "uf")
        lin(UH, [("gm", "id8k")] + USED)
        for i in range(3):
            tt(E[i], blk("mall", i), UU, A.is_equal)
        if OPT["un"] == 0 and not last:
            act("uf", UU, IDN, bias=LIFT)
            put(G("tool", jl), "uf")
        lin(MARK, [("gm", "id2k")] + [("idn8m", x) for x in E])
        lin(AUP, [("id8k", x) for x in E], sp=False)
        if t:
            ts("q2c%d" % t, blk(qa, 2), NOIDX, None, A.bitwise_and)
            tt(P01, blk(qa, 0), blk(qa, 1), A.max)
        above(OPT["ohu"][t], "ohu", UH, 8192.0)
        tt("qv", P01, q2, A.max)
        ts("mv", "qv", MSK, None, A.bitwise_and)
        tt("g1%d" % t, "qv", MARK, A.add)
        give(t, "g1%d" % t, q2, "land" if last else blk("qa%d" % (t + 1), 2))
        tt("omv", "mv", OH, A.mult)
        mm(AUP, "idb", "omv", False, True)
        tt("x1", "ohu", MARK, A.max)
        tt("al", P01, blk(qa, 0), A.not_equal)
        tt("be", P01, q2, A.is_gt)
        if OPT["sc"] == 1:
            changes(SC)
        if not ahead:
            jobs()
        if OPT["sc"] == 3:
            changes(SUM)
            if not last and not ahead:
                table()
        tt("vh", "x1", AUP, A.min)
        for b in range(3):
            differences(b)
        lin(VL, [("idb", "dm"), ("bo", "vh")])
        lin(ZL, [("idb", "dm"), ("bo", "vh")], sp=False)
        least("vs", VL)
        if not last:
            if OPT["nfirst"][t] == "n":
                next_list(t + 1)
                long_gather("ng", "nxt", 128, 0, EARLY[t + 1])
            tool_list(t + 1)
            limits(t + 1)
            long_gather("sg", "sdt", 0, 0, SOON[t + 1])
            if OPT["ex"]:
                mm(LT, "lg", "idb", True, True)
                act("lgt", LT)
        lin(SR, [("id2k", "cn15"), ("bo", "x1")])
        earlier(0)
        differences(3)
        earlier(1)
        to_list(lst("vl", t), "vs")
        if OPT["sc"] == 0:
            changes(SUM)
        earlier(2)
        earlier(3)
        new_pairs(t)
        ts("shf", SR, R("rtn", t, t + 1), 8.0, A.max, A.min)
        if not last and OPT["nfirst"][t] != "n":
            next_list(t + 1)
            long_gather("ng", "nxt", 128, 0, EARLY[t + 1])
        tt("yy", G(XW, lst("vl", t)), "shf", A.subtract)
        def finish():
            tt("y1", R(NP, 0, 256), blk(qa, 0, 2), A.max)
            act("un", "y1", IDN, LIFT - 0.36, 1 / 8192)
            mm(R(NQ, 0, 256), TWO, R("ends", rows=2), True, False)
            mm(R(NQ, 0, 256), "idn1m", "ss", False, False)
            mm(R(NQ, 0, 256), "idn4k", "un", False, True)

        if last and OPT["fin"]:
            finish()
        least("os_", ZL)
        ts("yc", "yy", 0.0, 255.0, A.max, A.min)
        to_list(lst("ofl", t), "os_")
        if not last:
            cp(firsts(t + 1), AL)
            ts(nexts(t + 1), NL, LIFT, None, A.add)
        cp(G("xt", lst("ofl", t)), "yc")
        if last:
            store("y", T.yx[:, :], XW, "ox")
            if not OPT["fin"]:
                finish()
            ts("hi2", "land", 1, -4096, A.logical_shift_right, A.bitwise_and)
            ts("mv", "land", MSK, None, A.bitwise_and)
            tt("yo", R(NQ, 0, 256), "y1", A.add)
            store("s", T.yp[:, 0:256], R("yo"), "op")
            tt("y3", "hi2", "mv", A.add)
            store("y", T.yp[:, 256:384], R("y3"), "oq")
        else:
            for b in range(4):
                spread(t + 1, b)
    issue()
    for sem in ("sv", "ss", "sp", "sg"):
        g.wait_ge(T.sem[sem], cnt[sem])
    g.wait_ge(T.sem.sent, NT * len(topo.engines(core, nxt_core)))
    for sem in ("ox", "op", "oq"):
        g.wait_ge(T.sem[sem], 16)
